import numpy as np
import ml_dtypes


def mxq(x, axis, fmt="e4m3"):
    dtype, down = {"e4m3": (ml_dtypes.float8_e4m3fn, 7), "e5m2": (ml_dtypes.float8_e5m2, 14)}[fmt]
    v = np.moveaxis(np.asarray(x, np.float32).astype(ml_dtypes.bfloat16).astype(np.float64), axis, -1)
    blocks = v.reshape(v.shape[:-1] + (-1, 32))
    amax = np.abs(blocks).max(-1, keepdims=True)
    byte = np.maximum(np.where(amax > 0, np.frexp(amax)[1] - 1 + 127, 0) - down, 1)
    scale = np.exp2(byte - 127.0)
    codes = (blocks / scale).astype(np.float32).astype(dtype).astype(np.float64)
    return np.moveaxis((codes * scale).reshape(v.shape), -1, axis)


WIDE = False


def mx_kscale(k):
    if not WIDE:
        return np.ones(k)
    levels = np.array([10, -10, 5, -5, 0])
    if k % 512:
        return np.exp2(np.random.permutation(np.resize(levels, k // 32))).repeat(32)
    a = np.empty((k // 512, 16))
    for p in range(k // 512):
        a[p, :8] = np.random.permutation(np.resize(levels, 8))
        for g in range(8):
            far = levels[np.abs(levels - a[p, g]) >= 10]
            a[p, g + 8] = far[np.random.randint(len(far))]
    return np.exp2(a.ravel()).repeat(32)


def f64(x):
    return np.asarray(x).astype(np.float64)


def striped(idx):
    return np.tile(idx.reshape(-1, 16).T, (8, 1)).astype(np.uint16)


def unstriped(offs):
    return offs[:16].T.reshape(-1).astype(np.int64)


def relu(v):
    return np.maximum(v, 0.0)


K, T, E, C, N = 1536, 768, 4, 128, 512


def by_expert(wq, xq):
    return np.concatenate([wq[e].T @ xq[:, e * C:(e + 1) * C] for e in range(E)], axis=1)


def setup_inputs():
    n = np.random.standard_normal
    s = mx_kscale(K)[:, None]
    return {
        "xT": (n((K, T)) * s).astype(np.float32),
        "w": (n((E, K, N)) / np.sqrt(K) / s[None]).astype(np.float32),
        "b": (0.3 * n((N, E))).astype(np.float32),
        "gate": np.tile(np.random.uniform(0.2, 1.0, E * C), (N, 1)).astype(np.float32),
        "offs": striped(np.random.permutation(T)[:E * C]),
    }


def reference(xT, w, b, gate, offs):
    idx = unstriped(offs)
    xq = mxq(f64(xT)[:, idx], 0, "e4m3")
    y = by_expert(mxq(f64(w), 1, "e4m3"), xq)
    y = relu(y + np.repeat(f64(b), C, axis=1))
    out = np.zeros((N, T))
    out[:, idx] = f64(gate) * y
    return out

@@ -1,0 +1,150 @@
+from contextlib import ExitStack
+
+import concourse.mybir as mybir
+
+K, T, E, C, N = 1536, 768, 4, 128, 512
+P = 128
+PACK = 4
+A = K // (P * PACK)
+S = E * C
+M = N // P
+
+FLOPS = 2 * K * N * S
+BYTES = 4 * (K * T + E * K * N + N * E + P * S + N * T) + 2 * P * (S // 16)
+
+F32 = mybir.dt.float32
+BF16 = mybir.dt.bfloat16
+U32 = mybir.dt.uint32
+U16 = mybir.dt.uint16
+U8 = mybir.dt.uint8
+FP8X4 = mybir.dt.float8_e4m3fn_x4
+RELU = mybir.ActivationFunctionType.Relu
+X_PIECES = (((0, 48, 128), (128, 176, 256), (256, 512, 768)), ((0, 384, 768),))
+W_PIECES = {(e, a): (((0, 160, 256), (256, 416, 512)) if a == 2 else ((0, 448, 512),)) for e in range(E) for a in range(A)}
+PUT_AFTER = (4, 4)
+MULT = mybir.AluOpType.mult
+
+
+def lay_side_by_side(copy, grouped, raw, lo, hi):
+    copy(
+        out=grouped[:, lo:hi, :].rearrange("p (c i) t -> p c t i", i=4),
+        in_=raw[:, :, lo:hi].rearrange("p t (c i) -> p c t i", i=4),
+    )
+
+
+def tile_routed_moe_kernel(tc, xT, w, b, gate, offs, out):
+    nc = tc.nc
+    with ExitStack() as ctx:
+        keep = ctx.enter_context(tc.tile_pool(name="keep", bufs=1))
+        xstage = ctx.enter_context(tc.tile_pool(name="xstage", bufs=2))
+        wstage = ctx.enter_context(tc.tile_pool(name="wstage", bufs=3))
+        ypool = ctx.enter_context(tc.tile_pool(name="ypool", bufs=8))
+        psum = ctx.enter_context(tc.psum_pool(name="psum", bufs=2))
+
+        x_rows = xT.rearrange("(a p t) n -> a p t n", p=P, t=PACK)
+        w_rows = w.rearrange("e (a p t) n -> e a p t n", p=P, t=PACK)
+
+        offsets = keep.tile([P, S // 16], U16, name="offsets")
+        x_raw = [keep.tile([P, PACK, T], F32, name=f"x_raw{a}") for a in range(A)]
+        x_codes = [keep.tile([P, T], U32, name=f"x_codes{a}", align_bytes=64) for a in range(A)]
+        x_scales = keep.tile([P, T], U8, name="x_scales", align_bytes=64)
+        s_codes = [keep.tile([P, S], U32, name=f"s_codes{a}", align_bytes=64) for a in range(A)]
+        s_scales = keep.tile([P, S], U8, name="s_scales", align_bytes=64)
+        bias = keep.tile([P, M, E], F32, name="bias")
+        gates = keep.tile([P, S], F32, name="gates")
+        windows = [keep.tile([P, T], F32, name=f"window{m}") for m in range(M)]
+
+        w_raw = {}
+        w_codes = {}
+        w_scales = {}
+        for e in range(E):
+            for a in range(A):
+                w_raw[e, a] = keep.tile([P, PACK, N], F32, name=f"w_raw{e}_{a}")
+                w_codes[e, a] = keep.tile([P, N], U32, name=f"w_codes{e}_{a}", align_bytes=64)
+                w_scales[e, a] = keep.tile([P, N], U8, name=f"w_scales{e}_{a}", align_bytes=64)
+
+        nc.gpsimd.memset(x_scales[:], 0)
+        warm = keep.tile([P, 2], F32, name="warm")
+        nc.vector.memset(warm[:], 0.0)
+        nc.scalar.activation(out=warm[:, 1:2], in_=warm[:, 0:1], func=RELU)
+
+        for lo, hi in ((0, 128), (128, 256)):
+            nc.sync.dma_start(x_raw[0][:, :, lo:hi], x_rows[0, :, :, lo:hi])
+        nc.sync.dma_start(x_raw[0][:, :, 256:T], x_rows[0, :, :, 256:T])
+        nc.sync.dma_start(offsets[:], offs)
+        nc.sync.dma_start(x_raw[1][:], x_rows[1])
+        nc.sync.dma_start(x_raw[2][:], x_rows[2])
+        nc.sync.dma_start(bias[:], b.rearrange("(m p) e -> p m e", p=P))
+        for e in range(E):
+            for a in range(A):
+                if (e, a) == (E - 1, A - 1):
+                    for lo, hi in ((0, 256), (256, 512)):
+                        nc.sync.dma_start(w_raw[e, a][:, :, lo:hi], w_rows[e, a, :, :, lo:hi])
+                else:
+                    nc.sync.dma_start(w_raw[e, a][:], w_rows[e, a])
+                if (e, a) == (0, 0):
+                    nc.sync.dma_start(gates[:], gate[0:P, :])
+
+        for m in range(M):
+            nc.vector.memset(windows[m][:], 0.0)
+
+        for a in range(A):
+            grouped = xstage.tile([P, T, PACK], BF16, name="x_grouped", align_bytes=64)
+            pieces = X_PIECES[min(a, 1)]
+            for lo, mid, hi in pieces:
+                lay_side_by_side(nc.scalar.copy, grouped, x_raw[a], lo, mid)
+                lay_side_by_side(nc.vector.tensor_copy, grouped, x_raw[a], mid, hi)
+            for lo, hi in ((0, 256), (256, 768)):
+                nc.vector.quantize_mx(
+                    out=x_codes[a][:, lo:hi].bitcast(FP8X4),
+                    scales=x_scales[4 * a : P, lo:hi],
+                    in_=grouped[:, lo:hi, :].rearrange("p n t -> p (n t)"),
+                )
+            nc.vector.tensor_copy(s_codes[a][:], x_codes[a][:].indirect(offsets[:]))
+        nc.vector.tensor_copy(s_scales[:], x_scales[:].indirect(offsets[:]))
+
+        def put_back(e, m, y):
+            nc.vector.tensor_tensor(
+                windows[m][:].indirect(offsets[:, e * C // 16 : (e + 1) * C // 16]),
+                y[:],
+                gates[:, e * C : (e + 1) * C],
+                MULT,
+            )
+            if e == E - 1:
+                nc.sync.dma_start(out[m * P : (m + 1) * P, :], windows[m][:])
+
+        waiting = []
+        for e in range(E):
+            acc = [psum.tile([P, C], F32, name=f"acc{m}") for m in range(M)]
+            slots = slice(e * C, (e + 1) * C)
+            for a in range(A):
+                grouped = wstage.tile([P, N, PACK], BF16, name="w_grouped", align_bytes=64)
+                for lo, mid, hi in W_PIECES[e, a]:
+                    if mid > lo:
+                        lay_side_by_side(nc.scalar.copy, grouped, w_raw[e, a], lo, mid)
+                    if hi > mid:
+                        lay_side_by_side(nc.vector.tensor_copy, grouped, w_raw[e, a], mid, hi)
+                    nc.vector.quantize_mx(
+                        out=w_codes[e, a][:, lo:hi].bitcast(FP8X4),
+                        scales=w_scales[e, a][:, lo:hi],
+                        in_=grouped[:, lo:hi, :].rearrange("p n t -> p (n t)"),
+                    )
+                    for m in range(lo // P, hi // P):
+                        cols = slice(m * P, (m + 1) * P)
+                        nc.tensor.matmul_mx(
+                            out=acc[m][:],
+                            lhsT=w_codes[e, a][:, cols].bitcast(FP8X4),
+                            lhsT_scale=w_scales[e, a][:, cols],
+                            rhs=s_codes[a][:, slots].bitcast(FP8X4),
+                            rhs_scale=s_scales[4 * a : P, slots],
+                            start=(a == 0),
+                            stop=(a == A - 1),
+                        )
+                        if a == A - 1:
+                            y = ypool.tile([P, C], F32, name="y")
+                            nc.scalar.activation(out=y[:], in_=acc[m][:], func=RELU, bias=bias[:, m, e : e + 1], scale=1.0)
+                            waiting.append((e, m, y))
+                for job in [waiting.pop(0) for i in range(min(len(waiting), PUT_AFTER[a]))] if a < A - 1 else []:
+                    put_back(*job)
+        for job in waiting:
+            put_back(*job)

@@ -19,10 +19,17 @@ U16 = mybir.dt.uint16
 U8 = mybir.dt.uint8
 FP8X4 = mybir.dt.float8_e4m3fn_x4
 RELU = mybir.ActivationFunctionType.Relu
-X_PIECES = (((0, 48, 128), (128, 176, 256), (256, 512, 768)), ((0, 384, 768),))
-W_PIECES = {(e, a): (((0, 160, 256), (256, 416, 512)) if a == 2 else ((0, 448, 512),)) for e in range(E) for a in range(A)}
-PUT_AFTER = (4, 4)
 MULT = mybir.AluOpType.mult
+ADD = mybir.AluOpType.add
+X_PIECES = (((0, 48, 128), (128, 176, 256), (256, 512, 768)), ((0, 384, 768),), ((0, 384, 768),))
+X_LOADS = (((0, 128), (128, 256), (256, 768)), ((0, 768),), ((0, 768),))
+UNITS = (
+    (0, 0, 512, ((384, 128), (384, 128), (384, 128))),
+    (1, 0, 512, ((384, 128), (384, 128), (384, 128))),
+    (2, 0, 512, ((384, 128), (384, 128), (384, 128))),
+    (3, 0, 256, ((192, 64), (192, 64), (192, 64))),
+    (3, 256, 512, ((192, 64), (192, 64), (128, 0))),
+)
 
 
 def lay_side_by_side(copy, grouped, raw, lo, hi):
@@ -57,43 +64,39 @@ def tile_routed_moe_kernel(tc, xT, w, b, gate, offs, out):
         w_raw = {}
         w_codes = {}
         w_scales = {}
-        for e in range(E):
+        for u, (e, lo, hi, shares) in enumerate(UNITS):
             for a in range(A):
-                w_raw[e, a] = keep.tile([P, PACK, N], F32, name=f"w_raw{e}_{a}")
-                w_codes[e, a] = keep.tile([P, N], U32, name=f"w_codes{e}_{a}", align_bytes=64)
-                w_scales[e, a] = keep.tile([P, N], U8, name=f"w_scales{e}_{a}", align_bytes=64)
+                w_raw[u, a] = keep.tile([P, PACK, hi - lo], F32, name=f"w_raw{u}_{a}")
+                w_codes[u, a] = keep.tile([P, hi - lo], U32, name=f"w_codes{u}_{a}", align_bytes=64)
+                w_scales[u, a] = keep.tile([P, hi - lo], U8, name=f"w_scales{u}_{a}", align_bytes=64)
 
         nc.gpsimd.memset(x_scales[:], 0)
         warm = keep.tile([P, 2], F32, name="warm")
         nc.vector.memset(warm[:], 0.0)
         nc.scalar.activation(out=warm[:, 1:2], in_=warm[:, 0:1], func=RELU)
 
-        for lo, hi in ((0, 128), (128, 256)):
-            nc.sync.dma_start(x_raw[0][:, :, lo:hi], x_rows[0, :, :, lo:hi])
-        nc.sync.dma_start(x_raw[0][:, :, 256:T], x_rows[0, :, :, 256:T])
-        nc.sync.dma_start(offsets[:], offs)
-        nc.sync.dma_start(x_raw[1][:], x_rows[1])
-        nc.sync.dma_start(x_raw[2][:], x_rows[2])
-        nc.sync.dma_start(bias[:], b.rearrange("(m p) e -> p m e", p=P))
-        for e in range(E):
+        for a in range(A):
+            for lo, hi in X_LOADS[a]:
+                nc.sync.dma_start(x_raw[a][:, :, lo:hi], x_rows[a, :, :, lo:hi])
+            if a == 0:
+                nc.sync.dma_start(offsets[:], offs)
+        for u, (e, lo, hi, shares) in enumerate(UNITS):
             for a in range(A):
-                if (e, a) == (E - 1, A - 1):
-                    for lo, hi in ((0, 256), (256, 512)):
-                        nc.sync.dma_start(w_raw[e, a][:, :, lo:hi], w_rows[e, a, :, :, lo:hi])
-                else:
-                    nc.sync.dma_start(w_raw[e, a][:], w_rows[e, a])
-                if (e, a) == (0, 0):
-                    nc.sync.dma_start(gates[:], gate[0:P, :])
+                nc.sync.dma_start(w_raw[u, a][:], w_rows[e, a, :, :, lo:hi])
+            if u == 0:
+                nc.sync.dma_start(bias[:], b.rearrange("(m p) e -> p m e", p=P))
+                nc.sync.dma_start(gates[:], gate[0:P, :])
 
         for m in range(M):
             nc.vector.memset(windows[m][:], 0.0)
 
         for a in range(A):
             grouped = xstage.tile([P, T, PACK], BF16, name="x_grouped", align_bytes=64)
-            pieces = X_PIECES[min(a, 1)]
-            for lo, mid, hi in pieces:
-                lay_side_by_side(nc.scalar.copy, grouped, x_raw[a], lo, mid)
-                lay_side_by_side(nc.vector.tensor_copy, grouped, x_raw[a], mid, hi)
+            for lo, mid, hi in X_PIECES[a]:
+                if mid > lo:
+                    lay_side_by_side(nc.scalar.copy, grouped, x_raw[a], lo, mid)
+                if hi > mid:
+                    lay_side_by_side(nc.vector.tensor_copy, grouped, x_raw[a], mid, hi)
             for lo, hi in ((0, 256), (256, 768)):
                 nc.vector.quantize_mx(
                     out=x_codes[a][:, lo:hi].bitcast(FP8X4),
@@ -103,48 +106,62 @@ def tile_routed_moe_kernel(tc, xT, w, b, gate, offs, out):
             nc.vector.tensor_copy(s_codes[a][:], x_codes[a][:].indirect(offsets[:]))
         nc.vector.tensor_copy(s_scales[:], x_scales[:].indirect(offsets[:]))
 
-        def put_back(e, m, y):
-            nc.vector.tensor_tensor(
-                windows[m][:].indirect(offsets[:, e * C // 16 : (e + 1) * C // 16]),
-                y[:],
-                gates[:, e * C : (e + 1) * C],
-                MULT,
-            )
+        def put_back(e, m, y, gated):
+            slots = slice(e * C, (e + 1) * C)
+            place = windows[m][:].indirect(offsets[:, e * C // 16 : (e + 1) * C // 16])
+            if gated:
+                nc.vector.tensor_copy(place, y[:])
+            else:
+                nc.vector.tensor_tensor(place, y[:], gates[:, slots], MULT)
             if e == E - 1:
                 nc.sync.dma_start(out[m * P : (m + 1) * P, :], windows[m][:])
 
         waiting = []
-        for e in range(E):
-            acc = [psum.tile([P, C], F32, name=f"acc{m}") for m in range(M)]
+        for u, (e, lo, hi, shares) in enumerate(UNITS):
+            width = hi - lo
+            blocks = range(lo // P, hi // P)
+            acc = {m: psum.tile([P, C], F32, name=f"acc{m}") for m in blocks}
             slots = slice(e * C, (e + 1) * C)
+            done = []
             for a in range(A):
                 grouped = wstage.tile([P, N, PACK], BF16, name="w_grouped", align_bytes=64)
-                for lo, mid, hi in W_PIECES[e, a]:
-                    if mid > lo:
-                        lay_side_by_side(nc.scalar.copy, grouped, w_raw[e, a], lo, mid)
-                    if hi > mid:
-                        lay_side_by_side(nc.vector.tensor_copy, grouped, w_raw[e, a], mid, hi)
-                    nc.vector.quantize_mx(
-                        out=w_codes[e, a][:, lo:hi].bitcast(FP8X4),
-                        scales=w_scales[e, a][:, lo:hi],
-                        in_=grouped[:, lo:hi, :].rearrange("p n t -> p (n t)"),
+                on_scalar, on_gpsimd = shares[a]
+                if on_scalar > 0:
+                    lay_side_by_side(nc.scalar.copy, grouped, w_raw[u, a], 0, on_scalar)
+                if on_gpsimd > 0:
+                    cols = slice(on_scalar, on_scalar + on_gpsimd)
+                    nc.gpsimd.tensor_scalar(
+                        grouped[:, cols, :], w_raw[u, a][:, :, cols].rearrange("p t n -> p n t"), 1.0, 0.0, MULT, ADD
                     )
-                    for m in range(lo // P, hi // P):
-                        cols = slice(m * P, (m + 1) * P)
-                        nc.tensor.matmul_mx(
-                            out=acc[m][:],
-                            lhsT=w_codes[e, a][:, cols].bitcast(FP8X4),
-                            lhsT_scale=w_scales[e, a][:, cols],
-                            rhs=s_codes[a][:, slots].bitcast(FP8X4),
-                            rhs_scale=s_scales[4 * a : P, slots],
-                            start=(a == 0),
-                            stop=(a == A - 1),
-                        )
-                        if a == A - 1:
-                            y = ypool.tile([P, C], F32, name="y")
-                            nc.scalar.activation(out=y[:], in_=acc[m][:], func=RELU, bias=bias[:, m, e : e + 1], scale=1.0)
-                            waiting.append((e, m, y))
-                for job in [waiting.pop(0) for i in range(min(len(waiting), PUT_AFTER[a]))] if a < A - 1 else []:
-                    put_back(*job)
+                if on_scalar + on_gpsimd < width:
+                    lay_side_by_side(nc.vector.tensor_copy, grouped, w_raw[u, a], on_scalar + on_gpsimd, width)
+                nc.vector.quantize_mx(
+                    out=w_codes[u, a][:].bitcast(FP8X4),
+                    scales=w_scales[u, a][:],
+                    in_=grouped[:, 0:width, :].rearrange("p n t -> p (n t)"),
+                )
+                for m in blocks:
+                    cols = slice(m * P - lo, (m + 1) * P - lo)
+                    nc.tensor.matmul_mx(
+                        out=acc[m][:],
+                        lhsT=w_codes[u, a][:, cols].bitcast(FP8X4),
+                        lhsT_scale=w_scales[u, a][:, cols],
+                        rhs=s_codes[a][:, slots].bitcast(FP8X4),
+                        rhs_scale=s_scales[4 * a : P, slots],
+                        start=(a == 0),
+                        stop=(a == A - 1),
+                    )
+                    if a == A - 1:
+                        y = ypool.tile([P, C], F32, name="y")
+                        nc.scalar.activation(out=y[:], in_=acc[m][:], func=RELU, bias=bias[:, m, e : e + 1], scale=1.0)
+                        gated = u < 3
+                        if gated:
+                            z = ypool.tile([P, C], F32, name="z")
+                            nc.gpsimd.tensor_tensor(z[:], y[:], gates[:, slots], MULT)
+                            y = z
+                        done.append((e, m, y, gated))
+            for job in waiting:
+                put_back(*job)
+            waiting = done
         for job in waiting:
             put_back(*job)

@@ -20,16 +20,20 @@ U8 = mybir.dt.uint8
 FP8X4 = mybir.dt.float8_e4m3fn_x4
 RELU = mybir.ActivationFunctionType.Relu
 MULT = mybir.AluOpType.mult
-ADD = mybir.AluOpType.add
-X_PIECES = (((0, 48, 128), (128, 176, 256), (256, 512, 768)), ((0, 384, 768),), ((0, 384, 768),))
-X_LOADS = (((0, 128), (128, 256), (256, 768)), ((0, 768),), ((0, 768),))
+X_PIECES = (((0, 128, 128), (128, 256, 256), (256, 448, 768)), ((0, 256, 256), (256, 448, 768)), ((0, 256, 256), (256, 512, 512), (512, 608, 768)))
+X_LOADS = (((0, 128), (128, 256), (256, 768)), ((0, 256), (256, 768)), ((0, 256), (256, 512), (512, 768)))
+X_QUANT = (((0, 256), (256, 768)), ((0, 256), (256, 768)), ((0, 256), (256, 512), (512, 768)))
 UNITS = (
-    (0, 0, 512, ((384, 128), (384, 128), (384, 128))),
-    (1, 0, 512, ((384, 128), (384, 128), (384, 128))),
-    (2, 0, 512, ((384, 128), (384, 128), (384, 128))),
-    (3, 0, 256, ((192, 64), (192, 64), (192, 64))),
-    (3, 256, 512, ((192, 64), (192, 64), (128, 0))),
+    (0, 0, 256, (256, 256, 128)),
+    (0, 256, 512, (128, 256, 64)),
+    (1, 0, 256, (256, 256, 64)),
+    (1, 256, 512, (256, 256, 64)),
+    (2, 0, 256, (256, 256, 64)),
+    (2, 256, 512, (256, 256, 64)),
+    (3, 0, 256, (256, 256, 64)),
+    (3, 256, 512, (256, 256, 128)),
 )
+FIRST_SLOTS = 512
 
 
 def lay_side_by_side(copy, grouped, raw, lo, hi):
@@ -44,8 +48,7 @@ def tile_routed_moe_kernel(tc, xT, w, b, gate, offs, out):
     with ExitStack() as ctx:
         keep = ctx.enter_context(tc.tile_pool(name="keep", bufs=1))
         xstage = ctx.enter_context(tc.tile_pool(name="xstage", bufs=2))
-        wstage = ctx.enter_context(tc.tile_pool(name="wstage", bufs=3))
-        ypool = ctx.enter_context(tc.tile_pool(name="ypool", bufs=8))
+        wstage = ctx.enter_context(tc.tile_pool(name="wstage", bufs=4))
         psum = ctx.enter_context(tc.psum_pool(name="psum", bufs=2))
 
         x_rows = xT.rearrange("(a p t) n -> a p t n", p=P, t=PACK)
@@ -61,14 +64,15 @@ def tile_routed_moe_kernel(tc, xT, w, b, gate, offs, out):
         gates = keep.tile([P, S], F32, name="gates")
         windows = [keep.tile([P, T], F32, name=f"window{m}") for m in range(M)]
 
+        pieces = [(u, a) for u in range(len(UNITS)) for a in range(A)]
         w_raw = {}
         w_codes = {}
         w_scales = {}
-        for u, (e, lo, hi, shares) in enumerate(UNITS):
-            for a in range(A):
-                w_raw[u, a] = keep.tile([P, PACK, hi - lo], F32, name=f"w_raw{u}_{a}")
-                w_codes[u, a] = keep.tile([P, hi - lo], U32, name=f"w_codes{u}_{a}", align_bytes=64)
-                w_scales[u, a] = keep.tile([P, hi - lo], U8, name=f"w_scales{u}_{a}", align_bytes=64)
+        for u, a in pieces:
+            e, lo, hi, shares = UNITS[u]
+            w_raw[u, a] = keep.tile([P, PACK, hi - lo], F32, name=f"w_raw{u}_{a}")
+            w_codes[u, a] = keep.tile([P, hi - lo], U32, name=f"w_codes{u}_{a}", align_bytes=64)
+            w_scales[u, a] = keep.tile([P, hi - lo], U8, name=f"w_scales{u}_{a}", align_bytes=64)
 
         nc.gpsimd.memset(x_scales[:], 0)
         warm = keep.tile([P, 2], F32, name="warm")
@@ -80,15 +84,18 @@ def tile_routed_moe_kernel(tc, xT, w, b, gate, offs, out):
                 nc.sync.dma_start(x_raw[a][:, :, lo:hi], x_rows[a, :, :, lo:hi])
             if a == 0:
                 nc.sync.dma_start(offsets[:], offs)
-        for u, (e, lo, hi, shares) in enumerate(UNITS):
-            for a in range(A):
-                nc.sync.dma_start(w_raw[u, a][:], w_rows[e, a, :, :, lo:hi])
-            if u == 0:
+        for u, a in pieces:
+            e, lo, hi, shares = UNITS[u]
+            nc.sync.dma_start(w_raw[u, a][:], w_rows[e, a, :, :, lo:hi])
+            if (u, a) == (0, A - 1):
                 nc.sync.dma_start(bias[:], b.rearrange("(m p) e -> p m e", p=P))
                 nc.sync.dma_start(gates[:], gate[0:P, :])
 
         for m in range(M):
             nc.vector.memset(windows[m][:], 0.0)
+
+        def gather(picked, whole, lo, hi):
+            nc.vector.tensor_copy(picked[:, lo:hi], whole[:].indirect(offsets[:, lo // 16 : hi // 16]))
 
         for a in range(A):
             grouped = xstage.tile([P, T, PACK], BF16, name="x_grouped", align_bytes=64)
@@ -97,71 +104,72 @@ def tile_routed_moe_kernel(tc, xT, w, b, gate, offs, out):
                     lay_side_by_side(nc.scalar.copy, grouped, x_raw[a], lo, mid)
                 if hi > mid:
                     lay_side_by_side(nc.vector.tensor_copy, grouped, x_raw[a], mid, hi)
-            for lo, hi in ((0, 256), (256, 768)):
+            for lo, hi in X_QUANT[a]:
                 nc.vector.quantize_mx(
                     out=x_codes[a][:, lo:hi].bitcast(FP8X4),
                     scales=x_scales[4 * a : P, lo:hi],
                     in_=grouped[:, lo:hi, :].rearrange("p n t -> p (n t)"),
                 )
-            nc.vector.tensor_copy(s_codes[a][:], x_codes[a][:].indirect(offsets[:]))
-        nc.vector.tensor_copy(s_scales[:], x_scales[:].indirect(offsets[:]))
+            gather(s_codes[a], x_codes[a], 0, S if a < A - 1 else FIRST_SLOTS)
+        gather(s_scales, x_scales, 0, FIRST_SLOTS)
 
-        def put_back(e, m, y, gated):
+        staged = {}
+        acc = {}
+        results = []
+
+        def round_weights(u, a):
+            e, lo, hi, shares = UNITS[u]
+            staged[u, a] = wstage.tile([P, N, PACK], BF16, name="w_grouped", align_bytes=64)
+            if shares[a] > 0:
+                lay_side_by_side(nc.scalar.copy, staged[u, a], w_raw[u, a], 0, shares[a])
+            if shares[a] < hi - lo:
+                lay_side_by_side(nc.vector.tensor_copy, staged[u, a], w_raw[u, a], shares[a], hi - lo)
+
+        def multiply(u, a):
+            e, lo, hi, shares = UNITS[u]
             slots = slice(e * C, (e + 1) * C)
-            place = windows[m][:].indirect(offsets[:, e * C // 16 : (e + 1) * C // 16])
-            if gated:
-                nc.vector.tensor_copy(place, y[:])
-            else:
-                nc.vector.tensor_tensor(place, y[:], gates[:, slots], MULT)
+            nc.vector.quantize_mx(
+                out=w_codes[u, a][:].bitcast(FP8X4),
+                scales=w_scales[u, a][:],
+                in_=staged[u, a][:, 0 : hi - lo, :].rearrange("p n t -> p (n t)"),
+            )
+            for m in range(lo // P, hi // P):
+                cols = slice(m * P - lo, (m + 1) * P - lo)
+                if a == 0:
+                    acc[m] = psum.tile([P, C], F32, name=f"acc{m}")
+                nc.tensor.matmul_mx(
+                    out=acc[m][:],
+                    lhsT=w_codes[u, a][:, cols].bitcast(FP8X4),
+                    lhsT_scale=w_scales[u, a][:, cols],
+                    rhs=s_codes[a][:, slots].bitcast(FP8X4),
+                    rhs_scale=s_scales[4 * a : P, slots],
+                    start=(a == 0),
+                    stop=(a == A - 1),
+                )
+                if a == A - 1:
+                    if u + 1 < len(UNITS):
+                        y = w_raw[u + 1, 0][:, m - lo // P, 0:C]
+                    else:
+                        last = keep.tile([P, C], F32, name=f"y{m}")
+                        y = last[:]
+                    nc.scalar.activation(out=y, in_=acc[m][:], func=RELU, bias=bias[:, m, e : e + 1], scale=1.0)
+                    results.append((e, m, y))
+
+        for i, piece in enumerate(pieces):
+            round_weights(*piece)
+            if i > 0:
+                multiply(*pieces[i - 1])
+            if FIRST_SLOTS < S and piece == (1, 0):
+                gather(s_codes[A - 1], x_codes[A - 1], FIRST_SLOTS, S)
+                gather(s_scales, x_scales, FIRST_SLOTS, S)
+        multiply(*pieces[-1])
+
+        for e, m, y in results:
+            nc.vector.tensor_tensor(
+                windows[m][:].indirect(offsets[:, e * C // 16 : (e + 1) * C // 16]),
+                y,
+                gates[:, e * C : (e + 1) * C],
+                MULT,
+            )
             if e == E - 1:
                 nc.sync.dma_start(out[m * P : (m + 1) * P, :], windows[m][:])
-
-        waiting = []
-        for u, (e, lo, hi, shares) in enumerate(UNITS):
-            width = hi - lo
-            blocks = range(lo // P, hi // P)
-            acc = {m: psum.tile([P, C], F32, name=f"acc{m}") for m in blocks}
-            slots = slice(e * C, (e + 1) * C)
-            done = []
-            for a in range(A):
-                grouped = wstage.tile([P, N, PACK], BF16, name="w_grouped", align_bytes=64)
-                on_scalar, on_gpsimd = shares[a]
-                if on_scalar > 0:
-                    lay_side_by_side(nc.scalar.copy, grouped, w_raw[u, a], 0, on_scalar)
-                if on_gpsimd > 0:
-                    cols = slice(on_scalar, on_scalar + on_gpsimd)
-                    nc.gpsimd.tensor_scalar(
-                        grouped[:, cols, :], w_raw[u, a][:, :, cols].rearrange("p t n -> p n t"), 1.0, 0.0, MULT, ADD
-                    )
-                if on_scalar + on_gpsimd < width:
-                    lay_side_by_side(nc.vector.tensor_copy, grouped, w_raw[u, a], on_scalar + on_gpsimd, width)
-                nc.vector.quantize_mx(
-                    out=w_codes[u, a][:].bitcast(FP8X4),
-                    scales=w_scales[u, a][:],
-                    in_=grouped[:, 0:width, :].rearrange("p n t -> p (n t)"),
-                )
-                for m in blocks:
-                    cols = slice(m * P - lo, (m + 1) * P - lo)
-                    nc.tensor.matmul_mx(
-                        out=acc[m][:],
-                        lhsT=w_codes[u, a][:, cols].bitcast(FP8X4),
-                        lhsT_scale=w_scales[u, a][:, cols],
-                        rhs=s_codes[a][:, slots].bitcast(FP8X4),
-                        rhs_scale=s_scales[4 * a : P, slots],
-                        start=(a == 0),
-                        stop=(a == A - 1),
-                    )
-                    if a == A - 1:
-                        y = ypool.tile([P, C], F32, name="y")
-                        nc.scalar.activation(out=y[:], in_=acc[m][:], func=RELU, bias=bias[:, m, e : e + 1], scale=1.0)
-                        gated = u < 3
-                        if gated:
-                            z = ypool.tile([P, C], F32, name="z")
-                            nc.gpsimd.tensor_tensor(z[:], y[:], gates[:, slots], MULT)
-                            y = z
-                        done.append((e, m, y, gated))
-            for job in waiting:
-                put_back(*job)
-            waiting = done
-        for job in waiting:
-            put_back(*job)

@@ -20,20 +20,15 @@ U8 = mybir.dt.uint8
 FP8X4 = mybir.dt.float8_e4m3fn_x4
 RELU = mybir.ActivationFunctionType.Relu
 MULT = mybir.AluOpType.mult
-X_PIECES = (((0, 128, 128), (128, 256, 256), (256, 448, 768)), ((0, 256, 256), (256, 448, 768)), ((0, 256, 256), (256, 512, 512), (512, 608, 768)))
-X_LOADS = (((0, 128), (128, 256), (256, 768)), ((0, 256), (256, 768)), ((0, 256), (256, 512), (512, 768)))
-X_QUANT = (((0, 256), (256, 768)), ((0, 256), (256, 768)), ((0, 256), (256, 512), (512, 768)))
-UNITS = (
-    (0, 0, 256, (256, 256, 128)),
-    (0, 256, 512, (128, 256, 64)),
-    (1, 0, 256, (256, 256, 64)),
-    (1, 256, 512, (256, 256, 64)),
-    (2, 0, 256, (256, 256, 64)),
-    (2, 256, 512, (256, 256, 64)),
-    (3, 0, 256, (256, 256, 64)),
-    (3, 256, 512, (256, 256, 128)),
-)
-FIRST_SLOTS = 512
+ADD = mybir.AluOpType.add
+X_PIECES = (((0, 256, 256), (256, 384, 768)), ((0, 256, 256), (256, 384, 768)), ((0, 256, 256), (256, 384, 768)))
+X_LOADS = (((0, 768),), ((0, 768),), ((0, 768),))
+X_QUANT = (((0, 256), (256, 768)), ((0, 256), (256, 768)), ((0, 256), (256, 768)))
+W_LOADS = ((((0, 512),), ((0, 512),), ((0, 512),)), (((0, 512),), ((0, 512),), ((0, 512),)), (((0, 512),), ((0, 512),), ((0, 512),)), (((0, 512),), ((0, 512),), ((0, 256), (256, 512))))
+W_COPIES = (((("S", 0, 384), ("G", 384, 512)), (("S", 0, 384), ("G", 384, 512)), (("S", 0, 96), ("V", 96, 256), ("S", 256, 384), ("V", 384, 512))), ((("S", 0, 384), ("G", 384, 512)), (("S", 0, 384), ("G", 384, 512)), (("S", 0, 128), ("G", 128, 256), ("S", 256, 448), ("G", 448, 512))), ((("S", 0, 384), ("G", 384, 512)), (("S", 0, 384), ("G", 384, 512)), (("S", 0, 128), ("G", 128, 256), ("S", 256, 448), ("G", 448, 512))), ((("S", 0, 384), ("G", 384, 512)), (("S", 0, 384), ("G", 384, 512)), (("S", 0, 128), ("G", 128, 256), ("S", 256, 416), ("G", 416, 512))))
+W_QUANT = ((((0, 512),), ((0, 512),), ((0, 256), (256, 512))), (((0, 512),), ((0, 512),), ((0, 256), (256, 512))), (((0, 512),), ((0, 512),), ((0, 256), (256, 512))), (((0, 512),), ((0, 512),), ((0, 256), (256, 512))))
+GATED = 3
+Y_PLACE = (((-1, 0), (-1, 0), (-1, 0), (-1, 0)), ((-1, 0), (-1, 0), (-1, 0), (-1, 0)), ((-1, 0), (-1, 0), (-1, 0), (2, 0)))
 
 
 def lay_side_by_side(copy, grouped, raw, lo, hi):
@@ -64,15 +59,14 @@ def tile_routed_moe_kernel(tc, xT, w, b, gate, offs, out):
         gates = keep.tile([P, S], F32, name="gates")
         windows = [keep.tile([P, T], F32, name=f"window{m}") for m in range(M)]
 
-        pieces = [(u, a) for u in range(len(UNITS)) for a in range(A)]
+        pieces = [(e, a) for e in range(E) for a in range(A)]
         w_raw = {}
         w_codes = {}
         w_scales = {}
-        for u, a in pieces:
-            e, lo, hi, shares = UNITS[u]
-            w_raw[u, a] = keep.tile([P, PACK, hi - lo], F32, name=f"w_raw{u}_{a}")
-            w_codes[u, a] = keep.tile([P, hi - lo], U32, name=f"w_codes{u}_{a}", align_bytes=64)
-            w_scales[u, a] = keep.tile([P, hi - lo], U8, name=f"w_scales{u}_{a}", align_bytes=64)
+        for e, a in pieces:
+            w_raw[e, a] = keep.tile([P, PACK, N], F32, name=f"w_raw{e}_{a}")
+            w_codes[e, a] = keep.tile([P, N], U32, name=f"w_codes{e}_{a}", align_bytes=64)
+            w_scales[e, a] = keep.tile([P, N], U8, name=f"w_scales{e}_{a}", align_bytes=64)
 
         nc.gpsimd.memset(x_scales[:], 0)
         warm = keep.tile([P, 2], F32, name="warm")
@@ -84,10 +78,10 @@ def tile_routed_moe_kernel(tc, xT, w, b, gate, offs, out):
                 nc.sync.dma_start(x_raw[a][:, :, lo:hi], x_rows[a, :, :, lo:hi])
             if a == 0:
                 nc.sync.dma_start(offsets[:], offs)
-        for u, a in pieces:
-            e, lo, hi, shares = UNITS[u]
-            nc.sync.dma_start(w_raw[u, a][:], w_rows[e, a, :, :, lo:hi])
-            if (u, a) == (0, A - 1):
+        for e, a in pieces:
+            for lo, hi in W_LOADS[e][a]:
+                nc.sync.dma_start(w_raw[e, a][:, :, lo:hi], w_rows[e, a, :, :, lo:hi])
+            if (e, a) == (0, 1):
                 nc.sync.dma_start(bias[:], b.rearrange("(m p) e -> p m e", p=P))
                 nc.sync.dma_start(gates[:], gate[0:P, :])
 
@@ -110,66 +104,79 @@ def tile_routed_moe_kernel(tc, xT, w, b, gate, offs, out):
                     scales=x_scales[4 * a : P, lo:hi],
                     in_=grouped[:, lo:hi, :].rearrange("p n t -> p (n t)"),
                 )
-            gather(s_codes[a], x_codes[a], 0, S if a < A - 1 else FIRST_SLOTS)
-        gather(s_scales, x_scales, 0, FIRST_SLOTS)
+            gather(s_codes[a], x_codes[a], 0, S)
+        gather(s_scales, x_scales, 0, S)
 
         staged = {}
         acc = {}
         results = []
 
-        def round_weights(u, a):
-            e, lo, hi, shares = UNITS[u]
-            staged[u, a] = wstage.tile([P, N, PACK], BF16, name="w_grouped", align_bytes=64)
-            if shares[a] > 0:
-                lay_side_by_side(nc.scalar.copy, staged[u, a], w_raw[u, a], 0, shares[a])
-            if shares[a] < hi - lo:
-                lay_side_by_side(nc.vector.tensor_copy, staged[u, a], w_raw[u, a], shares[a], hi - lo)
+        def round_weights(e, a):
+            staged[e, a] = wstage.tile([P, N, PACK], BF16, name="w_grouped", align_bytes=64)
+            for engine, lo, hi in W_COPIES[e][a]:
+                if engine == "G":
+                    source = w_raw[e, a][:, :, lo:hi].rearrange("p t n -> p n t")
+                    nc.gpsimd.tensor_scalar(staged[e, a][:, lo:hi, :], source, 1.0, 0.0, MULT, ADD)
+                else:
+                    copy = nc.scalar.copy if engine == "S" else nc.vector.tensor_copy
+                    lay_side_by_side(copy, staged[e, a], w_raw[e, a], lo, hi)
 
-        def multiply(u, a):
-            e, lo, hi, shares = UNITS[u]
+        sums = {}
+
+        def empty_bank(e, m):
+            if e + 1 < E and Y_PLACE[e][m][0] >= 0:
+                later, first = Y_PLACE[e][m]
+                y = w_raw[e + 1, later][:, m, first : first + C]
+            else:
+                own = keep.tile([P, C], F32, name=f"y{e}_{m}")
+                y = own[:]
+            nc.scalar.activation(out=y, in_=sums[e, m][:], func=RELU, bias=bias[:, m, e : e + 1], scale=1.0)
+            if e < GATED:
+                gated = keep.tile([P, C], F32, name=f"gated{e}_{m}")
+                nc.gpsimd.tensor_tensor(gated[:], y, gates[:, e * C : (e + 1) * C], MULT)
+                y = gated[:]
+            results.append((e, m, y))
+
+        def multiply(e, a):
             slots = slice(e * C, (e + 1) * C)
-            nc.vector.quantize_mx(
-                out=w_codes[u, a][:].bitcast(FP8X4),
-                scales=w_scales[u, a][:],
-                in_=staged[u, a][:, 0 : hi - lo, :].rearrange("p n t -> p (n t)"),
-            )
-            for m in range(lo // P, hi // P):
-                cols = slice(m * P - lo, (m + 1) * P - lo)
-                if a == 0:
-                    acc[m] = psum.tile([P, C], F32, name=f"acc{m}")
-                nc.tensor.matmul_mx(
-                    out=acc[m][:],
-                    lhsT=w_codes[u, a][:, cols].bitcast(FP8X4),
-                    lhsT_scale=w_scales[u, a][:, cols],
-                    rhs=s_codes[a][:, slots].bitcast(FP8X4),
-                    rhs_scale=s_scales[4 * a : P, slots],
-                    start=(a == 0),
-                    stop=(a == A - 1),
+            for lo, hi in W_QUANT[e][a]:
+                nc.vector.quantize_mx(
+                    out=w_codes[e, a][:, lo:hi].bitcast(FP8X4),
+                    scales=w_scales[e, a][:, lo:hi],
+                    in_=staged[e, a][:, lo:hi, :].rearrange("p n t -> p (n t)"),
                 )
-                if a == A - 1:
-                    if u + 1 < len(UNITS):
-                        y = w_raw[u + 1, 0][:, m - lo // P, 0:C]
-                    else:
-                        last = keep.tile([P, C], F32, name=f"y{m}")
-                        y = last[:]
-                    nc.scalar.activation(out=y, in_=acc[m][:], func=RELU, bias=bias[:, m, e : e + 1], scale=1.0)
-                    results.append((e, m, y))
+                for m in range(lo // P, hi // P):
+                    cols = slice(m * P, (m + 1) * P)
+                    if a == 0:
+                        acc[m] = psum.tile([P, C], F32, name=f"acc{m}")
+                    nc.tensor.matmul_mx(
+                        out=acc[m][:],
+                        lhsT=w_codes[e, a][:, cols].bitcast(FP8X4),
+                        lhsT_scale=w_scales[e, a][:, cols],
+                        rhs=s_codes[a][:, slots].bitcast(FP8X4),
+                        rhs_scale=s_scales[4 * a : P, slots],
+                        start=(a == 0),
+                        stop=(a == A - 1),
+                    )
+                    if a == A - 1:
+                        sums[e, m] = acc[m]
+                        if e + 1 == E or Y_PLACE[e][m][0] <= 0:
+                            empty_bank(e, m)
 
         for i, piece in enumerate(pieces):
             round_weights(*piece)
+            for m in range(M):
+                if piece[0] > 0 and piece[1] > 0 and Y_PLACE[piece[0] - 1][m][0] == piece[1]:
+                    empty_bank(piece[0] - 1, m)
             if i > 0:
                 multiply(*pieces[i - 1])
-            if FIRST_SLOTS < S and piece == (1, 0):
-                gather(s_codes[A - 1], x_codes[A - 1], FIRST_SLOTS, S)
-                gather(s_scales, x_scales, FIRST_SLOTS, S)
         multiply(*pieces[-1])
 
         for e, m, y in results:
-            nc.vector.tensor_tensor(
-                windows[m][:].indirect(offsets[:, e * C // 16 : (e + 1) * C // 16]),
-                y,
-                gates[:, e * C : (e + 1) * C],
-                MULT,
-            )
+            place = windows[m][:].indirect(offsets[:, e * C // 16 : (e + 1) * C // 16])
+            if e < GATED:
+                nc.vector.tensor_copy(place, y)
+            else:
+                nc.vector.tensor_tensor(place, y, gates[:, e * C : (e + 1) * C], MULT)
             if e == E - 1:
                 nc.sync.dma_start(out[m * P : (m + 1) * P, :], windows[m][:])

@@ -10,7 +10,7 @@ S = E * C
 M = N // P
 
 FLOPS = 2 * K * N * S
-BYTES = 4 * (K * T + E * K * N + N * E + P * S + N * T) + 2 * P * (S // 16)
+BYTES = 4 * (K * T + E * K * N + N * E + S + N * T) + 2 * P * (S // 16)
 
 F32 = mybir.dt.float32
 BF16 = mybir.dt.bfloat16
@@ -20,15 +20,13 @@ U8 = mybir.dt.uint8
 FP8X4 = mybir.dt.float8_e4m3fn_x4
 RELU = mybir.ActivationFunctionType.Relu
 MULT = mybir.AluOpType.mult
-ADD = mybir.AluOpType.add
 X_PIECES = (((0, 256, 256), (256, 384, 768)), ((0, 256, 256), (256, 384, 768)), ((0, 256, 256), (256, 384, 768)))
 X_LOADS = (((0, 768),), ((0, 768),), ((0, 768),))
 X_QUANT = (((0, 256), (256, 768)), ((0, 256), (256, 768)), ((0, 256), (256, 768)))
 W_LOADS = ((((0, 512),), ((0, 512),), ((0, 512),)), (((0, 512),), ((0, 512),), ((0, 512),)), (((0, 512),), ((0, 512),), ((0, 512),)), (((0, 512),), ((0, 512),), ((0, 256), (256, 512))))
-W_COPIES = (((("S", 0, 384), ("G", 384, 512)), (("S", 0, 384), ("G", 384, 512)), (("S", 0, 96), ("V", 96, 256), ("S", 256, 384), ("V", 384, 512))), ((("S", 0, 384), ("G", 384, 512)), (("S", 0, 384), ("G", 384, 512)), (("S", 0, 128), ("G", 128, 256), ("S", 256, 448), ("G", 448, 512))), ((("S", 0, 384), ("G", 384, 512)), (("S", 0, 384), ("G", 384, 512)), (("S", 0, 128), ("G", 128, 256), ("S", 256, 448), ("G", 448, 512))), ((("S", 0, 384), ("G", 384, 512)), (("S", 0, 384), ("G", 384, 512)), (("S", 0, 128), ("G", 128, 256), ("S", 256, 416), ("G", 416, 512))))
+W_COPIES = (((("S", 0, 384), ("V", 384, 512)), (("S", 0, 384), ("V", 384, 512)), (("S", 0, 96), ("V", 96, 256), ("S", 256, 384), ("V", 384, 512))), ((("S", 0, 512),), (("S", 0, 320), ("V", 320, 512)), (("S", 0, 128), ("V", 128, 256), ("S", 256, 512))), ((("S", 0, 512),), (("S", 0, 320), ("V", 320, 512)), (("S", 0, 128), ("V", 128, 256), ("S", 256, 512))), ((("S", 0, 512),), (("S", 0, 320), ("V", 320, 512)), (("S", 0, 128), ("V", 128, 256), ("S", 256, 416), ("V", 416, 512))))
 W_QUANT = ((((0, 512),), ((0, 512),), ((0, 256), (256, 512))), (((0, 512),), ((0, 512),), ((0, 256), (256, 512))), (((0, 512),), ((0, 512),), ((0, 256), (256, 512))), (((0, 512),), ((0, 512),), ((0, 256), (256, 512))))
-GATED = 3
-Y_PLACE = (((-1, 0), (-1, 0), (-1, 0), (-1, 0)), ((-1, 0), (-1, 0), (-1, 0), (-1, 0)), ((-1, 0), (-1, 0), (-1, 0), (2, 0)))
+Y_PLACE = (((-1, 0), (-1, 0), (-1, 0), (2, 0)), ((-1, 0), (-1, 0), (-1, 0), (2, 0)), ((-1, 0), (-1, 0), (-1, 0), (2, 0)))
 
 
 def lay_side_by_side(copy, grouped, raw, lo, hi):
@@ -68,7 +66,11 @@ def tile_routed_moe_kernel(tc, xT, w, b, gate, offs, out):
             w_codes[e, a] = keep.tile([P, N], U32, name=f"w_codes{e}_{a}", align_bytes=64)
             w_scales[e, a] = keep.tile([P, N], U8, name=f"w_scales{e}_{a}", align_bytes=64)
 
+        gate_row = keep.tile([P, S], F32, name="gate_row")
+        ones = keep.tile([P, P], F32, name="ones")
         nc.gpsimd.memset(x_scales[:], 0)
+        nc.gpsimd.memset(gate_row[:], 0.0)
+        nc.gpsimd.memset(ones[:], 1.0)
         warm = keep.tile([P, 2], F32, name="warm")
         nc.vector.memset(warm[:], 0.0)
         nc.scalar.activation(out=warm[:, 1:2], in_=warm[:, 0:1], func=RELU)
@@ -78,15 +80,19 @@ def tile_routed_moe_kernel(tc, xT, w, b, gate, offs, out):
                 nc.sync.dma_start(x_raw[a][:, :, lo:hi], x_rows[a, :, :, lo:hi])
             if a == 0:
                 nc.sync.dma_start(offsets[:], offs)
+                nc.sync.dma_start(gate_row[0:1, :], gate[0:1, :])
         for e, a in pieces:
             for lo, hi in W_LOADS[e][a]:
                 nc.sync.dma_start(w_raw[e, a][:, :, lo:hi], w_rows[e, a, :, :, lo:hi])
             if (e, a) == (0, 1):
                 nc.sync.dma_start(bias[:], b.rearrange("(m p) e -> p m e", p=P))
-                nc.sync.dma_start(gates[:], gate[0:P, :])
 
         for m in range(M):
             nc.vector.memset(windows[m][:], 0.0)
+
+        spread = psum.tile([P, S], F32, name="acc0")
+        nc.tensor.matmul(spread[:], ones[:], gate_row[:], start=True, stop=True)
+        nc.scalar.copy(gates[:], spread[:])
 
         def gather(picked, whole, lo, hi):
             nc.vector.tensor_copy(picked[:, lo:hi], whole[:].indirect(offsets[:, lo // 16 : hi // 16]))
@@ -114,12 +120,8 @@ def tile_routed_moe_kernel(tc, xT, w, b, gate, offs, out):
         def round_weights(e, a):
             staged[e, a] = wstage.tile([P, N, PACK], BF16, name="w_grouped", align_bytes=64)
             for engine, lo, hi in W_COPIES[e][a]:
-                if engine == "G":
-                    source = w_raw[e, a][:, :, lo:hi].rearrange("p t n -> p n t")
-                    nc.gpsimd.tensor_scalar(staged[e, a][:, lo:hi, :], source, 1.0, 0.0, MULT, ADD)
-                else:
-                    copy = nc.scalar.copy if engine == "S" else nc.vector.tensor_copy
-                    lay_side_by_side(copy, staged[e, a], w_raw[e, a], lo, hi)
+                copy = nc.scalar.copy if engine == "S" else nc.vector.tensor_copy
+                lay_side_by_side(copy, staged[e, a], w_raw[e, a], lo, hi)
 
         sums = {}
 
@@ -131,10 +133,6 @@ def tile_routed_moe_kernel(tc, xT, w, b, gate, offs, out):
                 own = keep.tile([P, C], F32, name=f"y{e}_{m}")
                 y = own[:]
             nc.scalar.activation(out=y, in_=sums[e, m][:], func=RELU, bias=bias[:, m, e : e + 1], scale=1.0)
-            if e < GATED:
-                gated = keep.tile([P, C], F32, name=f"gated{e}_{m}")
-                nc.gpsimd.tensor_tensor(gated[:], y, gates[:, e * C : (e + 1) * C], MULT)
-                y = gated[:]
             results.append((e, m, y))
 
         def multiply(e, a):
@@ -173,10 +171,11 @@ def tile_routed_moe_kernel(tc, xT, w, b, gate, offs, out):
         multiply(*pieces[-1])
 
         for e, m, y in results:
-            place = windows[m][:].indirect(offsets[:, e * C // 16 : (e + 1) * C // 16])
-            if e < GATED:
-                nc.vector.tensor_copy(place, y)
-            else:
-                nc.vector.tensor_tensor(place, y, gates[:, e * C : (e + 1) * C], MULT)
+            nc.vector.tensor_tensor(
+                windows[m][:].indirect(offsets[:, e * C // 16 : (e + 1) * C // 16]),
+                y,
+                gates[:, e * C : (e + 1) * C],
+                MULT,
+            )
             if e == E - 1:
                 nc.sync.dma_start(out[m * P : (m + 1) * P, :], windows[m][:])

@@ -24,8 +24,8 @@ X_PIECES = (((0, 256, 256), (256, 384, 768)), ((0, 256, 256), (256, 384, 768)), 
 X_LOADS = (((0, 768),), ((0, 768),), ((0, 768),))
 X_QUANT = (((0, 256), (256, 768)), ((0, 256), (256, 768)), ((0, 256), (256, 768)))
 W_LOADS = ((((0, 512),), ((0, 512),), ((0, 512),)), (((0, 512),), ((0, 512),), ((0, 512),)), (((0, 512),), ((0, 512),), ((0, 512),)), (((0, 512),), ((0, 512),), ((0, 256), (256, 512))))
-W_COPIES = (((("S", 0, 384), ("V", 384, 512)), (("S", 0, 384), ("V", 384, 512)), (("S", 0, 96), ("V", 96, 256), ("S", 256, 384), ("V", 384, 512))), ((("S", 0, 512),), (("S", 0, 320), ("V", 320, 512)), (("S", 0, 128), ("V", 128, 256), ("S", 256, 512))), ((("S", 0, 512),), (("S", 0, 320), ("V", 320, 512)), (("S", 0, 128), ("V", 128, 256), ("S", 256, 512))), ((("S", 0, 512),), (("S", 0, 320), ("V", 320, 512)), (("S", 0, 128), ("V", 128, 256), ("S", 256, 416), ("V", 416, 512))))
-W_QUANT = ((((0, 512),), ((0, 512),), ((0, 256), (256, 512))), (((0, 512),), ((0, 512),), ((0, 256), (256, 512))), (((0, 512),), ((0, 512),), ((0, 256), (256, 512))), (((0, 512),), ((0, 512),), ((0, 256), (256, 512))))
+W_COPIES = (((("S", 0, 512),), (("S", 0, 384), ("V", 384, 512)), (("S", 0, 96), ("V", 96, 256), ("S", 256, 384), ("V", 384, 512))), ((("S", 0, 512),), (("S", 0, 256), ("S", 256, 320), ("V", 320, 512)), (("S", 0, 128), ("V", 128, 256), ("S", 256, 512))), ((("S", 0, 512),), (("S", 0, 256), ("S", 256, 320), ("V", 320, 512)), (("S", 0, 128), ("V", 128, 256), ("S", 256, 512))), ((("S", 0, 512),), (("S", 0, 256), ("S", 256, 320), ("V", 320, 512)), (("S", 0, 128), ("V", 128, 256), ("S", 256, 512))))
+W_QUANT = ((((0, 512),), ((0, 512),), ((0, 256), (256, 512))), (((0, 512),), ((0, 256), (256, 512)), ((0, 256), (256, 512))), (((0, 512),), ((0, 256), (256, 512)), ((0, 256), (256, 512))), (((0, 512),), ((0, 256), (256, 512)), ((0, 256), (256, 512))))
 Y_PLACE = (((-1, 0), (-1, 0), (-1, 0), (2, 0)), ((-1, 0), (-1, 0), (-1, 0), (2, 0)), ((-1, 0), (-1, 0), (-1, 0), (2, 0)))
 
 
@@ -53,7 +53,7 @@ def tile_routed_moe_kernel(tc, xT, w, b, gate, offs, out):
         x_scales = keep.tile([P, T], U8, name="x_scales", align_bytes=64)
         s_codes = [keep.tile([P, S], U32, name=f"s_codes{a}", align_bytes=64) for a in range(A)]
         s_scales = keep.tile([P, S], U8, name="s_scales", align_bytes=64)
-        bias = keep.tile([P, M, E], F32, name="bias")
+        bias = keep.tile([P, M, 2 * E], F32, name="bias")
         gates = keep.tile([P, S], F32, name="gates")
         windows = [keep.tile([P, T], F32, name=f"window{m}") for m in range(M)]
 
@@ -68,24 +68,22 @@ def tile_routed_moe_kernel(tc, xT, w, b, gate, offs, out):
 
         gate_row = keep.tile([P, S], F32, name="gate_row")
         ones = keep.tile([P, P], F32, name="ones")
-        nc.gpsimd.memset(x_scales[:], 0)
         nc.gpsimd.memset(gate_row[:], 0.0)
-        nc.gpsimd.memset(ones[:], 1.0)
-        warm = keep.tile([P, 2], F32, name="warm")
-        nc.vector.memset(warm[:], 0.0)
-        nc.scalar.activation(out=warm[:, 1:2], in_=warm[:, 0:1], func=RELU)
+        nc.gpsimd.memset(x_scales[:], 0)
+        nc.scalar.activation(out=ones[:], in_=gate_row[:, 0:P], func=RELU, bias=1.0, scale=1.0)
 
         for a in range(A):
             for lo, hi in X_LOADS[a]:
                 nc.sync.dma_start(x_raw[a][:, :, lo:hi], x_rows[a, :, :, lo:hi])
             if a == 0:
                 nc.sync.dma_start(offsets[:], offs)
+            if a == 1:
                 nc.sync.dma_start(gate_row[0:1, :], gate[0:1, :])
         for e, a in pieces:
             for lo, hi in W_LOADS[e][a]:
                 nc.sync.dma_start(w_raw[e, a][:, :, lo:hi], w_rows[e, a, :, :, lo:hi])
             if (e, a) == (0, 1):
-                nc.sync.dma_start(bias[:], b.rearrange("(m p) e -> p m e", p=P))
+                nc.sync.dma_start(bias[:, :, 0:E], b.rearrange("(m p) e -> p m e", p=P))
 
         for m in range(M):
             nc.vector.memset(windows[m][:], 0.0)

@@ -20,16 +20,23 @@ U8 = mybir.dt.uint8
 FP8X4 = mybir.dt.float8_e4m3fn_x4
 RELU = mybir.ActivationFunctionType.Relu
 MULT = mybir.AluOpType.mult
-X_PIECES = (((0, 256, 256), (256, 384, 768)), ((0, 256, 256), (256, 384, 768)), ((0, 256, 256), (256, 384, 768)))
-X_LOADS = (((0, 768),), ((0, 768),), ((0, 768),))
-X_QUANT = (((0, 256), (256, 768)), ((0, 256), (256, 768)), ((0, 256), (256, 768)))
-W_LOADS = ((((0, 512),), ((0, 512),), ((0, 512),)), (((0, 512),), ((0, 512),), ((0, 512),)), (((0, 512),), ((0, 512),), ((0, 512),)), (((0, 512),), ((0, 512),), ((0, 256), (256, 512))))
-W_COPIES = (((("S", 0, 512),), (("S", 0, 384), ("V", 384, 512)), (("S", 0, 96), ("V", 96, 256), ("S", 256, 384), ("V", 384, 512))), ((("S", 0, 512),), (("S", 0, 256), ("S", 256, 320), ("V", 320, 512)), (("S", 0, 128), ("V", 128, 256), ("S", 256, 512))), ((("S", 0, 512),), (("S", 0, 256), ("S", 256, 320), ("V", 320, 512)), (("S", 0, 128), ("V", 128, 256), ("S", 256, 512))), ((("S", 0, 512),), (("S", 0, 256), ("S", 256, 320), ("V", 320, 512)), (("S", 0, 128), ("V", 128, 256), ("S", 256, 512))))
-W_QUANT = ((((0, 512),), ((0, 512),), ((0, 256), (256, 512))), (((0, 512),), ((0, 256), (256, 512)), ((0, 256), (256, 512))), (((0, 512),), ((0, 256), (256, 512)), ((0, 256), (256, 512))), (((0, 512),), ((0, 256), (256, 512)), ((0, 256), (256, 512))))
-Y_PLACE = (((-1, 0), (-1, 0), (-1, 0), (2, 0)), ((-1, 0), (-1, 0), (-1, 0), (2, 0)), ((-1, 0), (-1, 0), (-1, 0), (2, 0)))
+
+X_FIRST = 256
+X_QUANTISE = ((0, X_FIRST), (X_FIRST, T))
+X_COPIES = (("scalar", 0, X_FIRST), ("scalar", X_FIRST, T // 2), ("vector", T // 2, T))
+
+HALF, QUARTER = N // 2, N // 4
+W_COPIES = (
+    (("scalar", 0, N),),
+    (("scalar", 0, HALF), ("vector", HALF, N)),
+    (("scalar", 0, QUARTER), ("vector", QUARTER, HALF), ("scalar", HALF, N)),
+)
+W_QUANTISE = (((0, N),), ((0, HALF), (HALF, N)), ((0, HALF), (HALF, N)))
+LATE_BLOCK = M - 1
 
 
-def lay_side_by_side(copy, grouped, raw, lo, hi):
+def round_and_group(nc, engine, grouped, raw, lo, hi):
+    copy = nc.scalar.copy if engine == "scalar" else nc.vector.tensor_copy
     copy(
         out=grouped[:, lo:hi, :].rearrange("p (c i) t -> p c t i", i=4),
         in_=raw[:, :, lo:hi].rearrange("p t (c i) -> p c t i", i=4),
@@ -73,16 +80,18 @@ def tile_routed_moe_kernel(tc, xT, w, b, gate, offs, out):
         nc.scalar.activation(out=ones[:], in_=gate_row[:, 0:P], func=RELU, bias=1.0, scale=1.0)
 
         for a in range(A):
-            for lo, hi in X_LOADS[a]:
-                nc.sync.dma_start(x_raw[a][:, :, lo:hi], x_rows[a, :, :, lo:hi])
+            nc.sync.dma_start(x_raw[a][:], x_rows[a])
             if a == 0:
                 nc.sync.dma_start(offsets[:], offs)
             if a == 1:
                 nc.sync.dma_start(gate_row[0:1, :], gate[0:1, :])
         for e, a in pieces:
-            for lo, hi in W_LOADS[e][a]:
-                nc.sync.dma_start(w_raw[e, a][:, :, lo:hi], w_rows[e, a, :, :, lo:hi])
-            if (e, a) == (0, 1):
+            if (e, a) == pieces[-1]:
+                for lo, hi in ((0, HALF), (HALF, N)):
+                    nc.sync.dma_start(w_raw[e, a][:, :, lo:hi], w_rows[e, a, :, :, lo:hi])
+            else:
+                nc.sync.dma_start(w_raw[e, a][:], w_rows[e, a])
+            if (e, a) == (0, A - 2):
                 nc.sync.dma_start(bias[:, :, 0:E], b.rearrange("(m p) e -> p m e", p=P))
 
         for m in range(M):
@@ -92,41 +101,31 @@ def tile_routed_moe_kernel(tc, xT, w, b, gate, offs, out):
         nc.tensor.matmul(spread[:], ones[:], gate_row[:], start=True, stop=True)
         nc.scalar.copy(gates[:], spread[:])
 
-        def gather(picked, whole, lo, hi):
-            nc.vector.tensor_copy(picked[:, lo:hi], whole[:].indirect(offsets[:, lo // 16 : hi // 16]))
-
         for a in range(A):
-            grouped = xstage.tile([P, T, PACK], BF16, name="x_grouped", align_bytes=64)
-            for lo, mid, hi in X_PIECES[a]:
-                if mid > lo:
-                    lay_side_by_side(nc.scalar.copy, grouped, x_raw[a], lo, mid)
-                if hi > mid:
-                    lay_side_by_side(nc.vector.tensor_copy, grouped, x_raw[a], mid, hi)
-            for lo, hi in X_QUANT[a]:
+            x_grouped = xstage.tile([P, T, PACK], BF16, name="x_grouped", align_bytes=64)
+            for engine, lo, hi in X_COPIES:
+                round_and_group(nc, engine, x_grouped, x_raw[a], lo, hi)
+            for lo, hi in X_QUANTISE:
                 nc.vector.quantize_mx(
                     out=x_codes[a][:, lo:hi].bitcast(FP8X4),
-                    scales=x_scales[4 * a : P, lo:hi],
-                    in_=grouped[:, lo:hi, :].rearrange("p n t -> p (n t)"),
+                    scales=x_scales[PACK * a : P, lo:hi],
+                    in_=x_grouped[:, lo:hi, :].rearrange("p n t -> p (n t)"),
                 )
-            gather(s_codes[a], x_codes[a], 0, S)
-        gather(s_scales, x_scales, 0, S)
+            nc.vector.tensor_copy(s_codes[a][:], x_codes[a][:].indirect(offsets[:]))
+        nc.vector.tensor_copy(s_scales[:], x_scales[:].indirect(offsets[:]))
 
-        staged = {}
-        acc = {}
+        w_grouped = {}
+        sums = {}
         results = []
 
         def round_weights(e, a):
-            staged[e, a] = wstage.tile([P, N, PACK], BF16, name="w_grouped", align_bytes=64)
-            for engine, lo, hi in W_COPIES[e][a]:
-                copy = nc.scalar.copy if engine == "S" else nc.vector.tensor_copy
-                lay_side_by_side(copy, staged[e, a], w_raw[e, a], lo, hi)
-
-        sums = {}
+            w_grouped[e, a] = wstage.tile([P, N, PACK], BF16, name="w_grouped", align_bytes=64)
+            for engine, lo, hi in W_COPIES[a]:
+                round_and_group(nc, engine, w_grouped[e, a], w_raw[e, a], lo, hi)
 
         def empty_bank(e, m):
-            if e + 1 < E and Y_PLACE[e][m][0] >= 0:
-                later, first = Y_PLACE[e][m]
-                y = w_raw[e + 1, later][:, m, first : first + C]
+            if m == LATE_BLOCK and e + 1 < E:
+                y = w_raw[e + 1, A - 1][:, m, 0:C]
             else:
                 own = keep.tile([P, C], F32, name=f"y{e}_{m}")
                 y = own[:]
@@ -135,35 +134,32 @@ def tile_routed_moe_kernel(tc, xT, w, b, gate, offs, out):
 
         def multiply(e, a):
             slots = slice(e * C, (e + 1) * C)
-            for lo, hi in W_QUANT[e][a]:
+            for lo, hi in W_QUANTISE[a]:
                 nc.vector.quantize_mx(
                     out=w_codes[e, a][:, lo:hi].bitcast(FP8X4),
                     scales=w_scales[e, a][:, lo:hi],
-                    in_=staged[e, a][:, lo:hi, :].rearrange("p n t -> p (n t)"),
+                    in_=w_grouped[e, a][:, lo:hi, :].rearrange("p n t -> p (n t)"),
                 )
                 for m in range(lo // P, hi // P):
                     cols = slice(m * P, (m + 1) * P)
                     if a == 0:
-                        acc[m] = psum.tile([P, C], F32, name=f"acc{m}")
+                        sums[e, m] = psum.tile([P, C], F32, name=f"acc{m}")
                     nc.tensor.matmul_mx(
-                        out=acc[m][:],
+                        out=sums[e, m][:],
                         lhsT=w_codes[e, a][:, cols].bitcast(FP8X4),
                         lhsT_scale=w_scales[e, a][:, cols],
                         rhs=s_codes[a][:, slots].bitcast(FP8X4),
-                        rhs_scale=s_scales[4 * a : P, slots],
+                        rhs_scale=s_scales[PACK * a : P, slots],
                         start=(a == 0),
                         stop=(a == A - 1),
                     )
-                    if a == A - 1:
-                        sums[e, m] = acc[m]
-                        if e + 1 == E or Y_PLACE[e][m][0] <= 0:
-                            empty_bank(e, m)
+                    if a == A - 1 and (m != LATE_BLOCK or e == E - 1):
+                        empty_bank(e, m)
 
-        for i, piece in enumerate(pieces):
-            round_weights(*piece)
-            for m in range(M):
-                if piece[0] > 0 and piece[1] > 0 and Y_PLACE[piece[0] - 1][m][0] == piece[1]:
-                    empty_bank(piece[0] - 1, m)
+        for i, (e, a) in enumerate(pieces):
+            round_weights(e, a)
+            if e > 0 and a == A - 1:
+                empty_bank(e - 1, LATE_BLOCK)
             if i > 0:
                 multiply(*pieces[i - 1])
         multiply(*pieces[-1])

@@ -27,11 +27,11 @@ X_COPIES = (("scalar", 0, X_FIRST), ("scalar", X_FIRST, T // 2), ("vector", T //
 
 HALF, QUARTER = N // 2, N // 4
 W_COPIES = (
-    (("scalar", 0, N),),
     (("scalar", 0, HALF), ("vector", HALF, N)),
-    (("scalar", 0, QUARTER), ("vector", QUARTER, HALF), ("scalar", HALF, N)),
+    (("scalar", 0, N - QUARTER), ("vector", N - QUARTER, N)),
+    (("scalar", 0, HALF), ("scalar", HALF, N)),
 )
-W_QUANTISE = (((0, N),), ((0, HALF), (HALF, N)), ((0, HALF), (HALF, N)))
+W_QUANTISE = (((0, HALF), (HALF, N)),) * A
 LATE_BLOCK = M - 1
 
 
@@ -91,7 +91,7 @@ def tile_routed_moe_kernel(tc, xT, w, b, gate, offs, out):
                     nc.sync.dma_start(w_raw[e, a][:, :, lo:hi], w_rows[e, a, :, :, lo:hi])
             else:
                 nc.sync.dma_start(w_raw[e, a][:], w_rows[e, a])
-            if (e, a) == (0, A - 2):
+            if (e, a) == (0, A - 1):
                 nc.sync.dma_start(bias[:, :, 0:E], b.rearrange("(m p) e -> p m e", p=P))
 
         for m in range(M):
@@ -118,14 +118,13 @@ def tile_routed_moe_kernel(tc, xT, w, b, gate, offs, out):
         sums = {}
         results = []
 
-        def round_weights(e, a):
-            w_grouped[e, a] = wstage.tile([P, N, PACK], BF16, name="w_grouped", align_bytes=64)
-            for engine, lo, hi in W_COPIES[a]:
+        def round_weights(e, a, copies):
+            for engine, lo, hi in copies:
                 round_and_group(nc, engine, w_grouped[e, a], w_raw[e, a], lo, hi)
 
         def empty_bank(e, m):
             if m == LATE_BLOCK and e + 1 < E:
-                y = w_raw[e + 1, A - 1][:, m, 0:C]
+                y = w_raw[e + 1, 1][:, m, 0:C]
             else:
                 own = keep.tile([P, C], F32, name=f"y{e}_{m}")
                 y = own[:]
@@ -157,11 +156,14 @@ def tile_routed_moe_kernel(tc, xT, w, b, gate, offs, out):
                         empty_bank(e, m)
 
         for i, (e, a) in enumerate(pieces):
-            round_weights(e, a)
-            if e > 0 and a == A - 1:
-                empty_bank(e - 1, LATE_BLOCK)
+            copies = W_COPIES[a]
+            w_grouped[e, a] = wstage.tile([P, N, PACK], BF16, name="w_grouped", align_bytes=64)
+            round_weights(e, a, copies[:1])
             if i > 0:
                 multiply(*pieces[i - 1])
+            round_weights(e, a, copies[1:])
+            if e > 0 and a == 1:
+                empty_bank(e - 1, LATE_BLOCK)
         multiply(*pieces[-1])
 
         for e, m, y in results:

@@ -38,8 +38,8 @@ LATE_BLOCK = M - 1
 def round_and_group(nc, engine, grouped, raw, lo, hi):
     copy = nc.scalar.copy if engine == "scalar" else nc.vector.tensor_copy
     copy(
-        out=grouped[:, lo:hi, :].rearrange("p (c i) t -> p c t i", i=4),
-        in_=raw[:, :, lo:hi].rearrange("p t (c i) -> p c t i", i=4),
+        out=grouped[:, lo:hi, :].rearrange("p (c i) (u v) -> p c u i v", i=4, v=2),
+        in_=raw[:, :, lo:hi].rearrange("p (u v) (c i) -> p c u i v", i=4, v=2),
     )
 
 

@@ -26,10 +26,16 @@ X_QUANTISE = ((0, X_FIRST), (X_FIRST, T))
 X_COPIES = (("scalar", 0, X_FIRST), ("scalar", X_FIRST, T // 2), ("vector", T // 2, T))
 
 HALF, QUARTER = N // 2, N // 4
+MIDDLE_CUT = 320
 W_COPIES = (
     (("scalar", 0, HALF), ("vector", HALF, N)),
-    (("scalar", 0, N - QUARTER), ("vector", N - QUARTER, N)),
+    (("scalar", 0, MIDDLE_CUT), ("vector", MIDDLE_CUT, N)),
     (("scalar", 0, HALF), ("scalar", HALF, N)),
+)
+W_COPIES_FIRST = (
+    (("scalar", 0, HALF), ("scalar", HALF, N)),
+    W_COPIES[1],
+    (("scalar", 0, QUARTER), ("vector", QUARTER, HALF), ("scalar", HALF, N - QUARTER), ("vector", N - QUARTER, N)),
 )
 W_QUANTISE = (((0, HALF), (HALF, N)),) * A
 LATE_BLOCK = M - 1
@@ -156,7 +162,7 @@ def tile_routed_moe_kernel(tc, xT, w, b, gate, offs, out):
                         empty_bank(e, m)
 
         for i, (e, a) in enumerate(pieces):
-            copies = W_COPIES[a]
+            copies = (W_COPIES_FIRST if e == 0 else W_COPIES)[a]
             w_grouped[e, a] = wstage.tile([P, N, PACK], BF16, name="w_grouped", align_bytes=64)
             round_weights(e, a, copies[:1])
             if i > 0:

@@ -23,8 +23,10 @@ MULT = mybir.AluOpType.mult
 
 X_FIRST = 256
 X_QUANTISE = ((0, X_FIRST), (X_FIRST, T))
-X_COPIES = (("scalar", 0, X_FIRST), ("scalar", X_FIRST, T // 2), ("vector", T // 2, T))
+X_TAIL = T // 2 - X_FIRST
+X_COPIES = (("vector", 0, X_FIRST), ("scalar", X_FIRST, T - X_TAIL), ("vector", T - X_TAIL, T))
 
+HALVES = ((0, N // 2), (N // 2, N))
 HALF, QUARTER = N // 2, N // 4
 MIDDLE_CUT = 320
 W_COPIES = (
@@ -33,12 +35,12 @@ W_COPIES = (
     (("scalar", 0, HALF), ("scalar", HALF, N)),
 )
 W_COPIES_FIRST = (
-    (("scalar", 0, HALF), ("scalar", HALF, N)),
+    (("scalar", 0, N),),
     W_COPIES[1],
     (("scalar", 0, QUARTER), ("vector", QUARTER, HALF), ("scalar", HALF, N - QUARTER), ("vector", N - QUARTER, N)),
 )
-W_QUANTISE = (((0, HALF), (HALF, N)),) * A
 LATE_BLOCK = M - 1
+LATE_PASS = 1
 
 
 def round_and_group(nc, engine, grouped, raw, lo, hi):
@@ -93,7 +95,7 @@ def tile_routed_moe_kernel(tc, xT, w, b, gate, offs, out):
                 nc.sync.dma_start(gate_row[0:1, :], gate[0:1, :])
         for e, a in pieces:
             if (e, a) == pieces[-1]:
-                for lo, hi in ((0, HALF), (HALF, N)):
+                for lo, hi in HALVES:
                     nc.sync.dma_start(w_raw[e, a][:, :, lo:hi], w_rows[e, a, :, :, lo:hi])
             else:
                 nc.sync.dma_start(w_raw[e, a][:], w_rows[e, a])
@@ -130,7 +132,7 @@ def tile_routed_moe_kernel(tc, xT, w, b, gate, offs, out):
 
         def empty_bank(e, m):
             if m == LATE_BLOCK and e + 1 < E:
-                y = w_raw[e + 1, 1][:, m, 0:C]
+                y = w_raw[e + 1, LATE_PASS][:, m, 0:C]
             else:
                 own = keep.tile([P, C], F32, name=f"y{e}_{m}")
                 y = own[:]
@@ -139,7 +141,7 @@ def tile_routed_moe_kernel(tc, xT, w, b, gate, offs, out):
 
         def multiply(e, a):
             slots = slice(e * C, (e + 1) * C)
-            for lo, hi in W_QUANTISE[a]:
+            for lo, hi in HALVES:
                 nc.vector.quantize_mx(
                     out=w_codes[e, a][:, lo:hi].bitcast(FP8X4),
                     scales=w_scales[e, a][:, lo:hi],
@@ -168,7 +170,7 @@ def tile_routed_moe_kernel(tc, xT, w, b, gate, offs, out):
             if i > 0:
                 multiply(*pieces[i - 1])
             round_weights(e, a, copies[1:])
-            if e > 0 and a == 1:
+            if e > 0 and a == LATE_PASS:
                 empty_bank(e - 1, LATE_BLOCK)
         multiply(*pieces[-1])
 

@@ -1,6 +1,7 @@
 from contextlib import ExitStack
 
 import concourse.mybir as mybir
+from concourse.masks import make_identity
 
 K, T, E, C, N = 1536, 768, 4, 128, 512
 P = 128
@@ -24,7 +25,8 @@ MULT = mybir.AluOpType.mult
 X_FIRST = 256
 X_QUANTISE = ((0, X_FIRST), (X_FIRST, T))
 X_TAIL = T // 2 - X_FIRST
-X_COPIES = (("vector", 0, X_FIRST), ("scalar", X_FIRST, T - X_TAIL), ("vector", T - X_TAIL, T))
+X_TAILS = (X_TAIL + 64, X_TAIL, X_TAIL)
+X_COPIES = [(("vector", 0, X_FIRST), ("scalar", X_FIRST, T - tail), ("vector", T - tail, T)) for tail in X_TAILS]
 
 HALVES = ((0, N // 2), (N // 2, N))
 HALF, QUARTER = N // 2, N // 4
@@ -32,12 +34,14 @@ MIDDLE_CUT = 320
 W_COPIES = (
     (("scalar", 0, HALF), ("vector", HALF, N)),
     (("scalar", 0, MIDDLE_CUT), ("vector", MIDDLE_CUT, N)),
-    (("scalar", 0, HALF), ("scalar", HALF, N)),
+    (("scalar", 0, HALF), ("scalar", HALF, N - QUARTER), ("scalar", N - QUARTER, N)),
 )
+W_QUANTISE = (HALVES, HALVES, ((0, HALF), (HALF, N - QUARTER), (N - QUARTER, N)))
+SPLIT_LOADS = ((E - 2, A - 1), (E - 1, A - 1))
 W_COPIES_FIRST = (
     (("scalar", 0, N),),
     W_COPIES[1],
-    (("scalar", 0, QUARTER), ("vector", QUARTER, HALF), ("scalar", HALF, N - QUARTER), ("vector", N - QUARTER, N)),
+    (("scalar", 0, QUARTER), ("vector", QUARTER, HALF), ("scalar", HALF, N)),
 )
 LATE_BLOCK = M - 1
 LATE_PASS = 1
@@ -68,7 +72,7 @@ def tile_routed_moe_kernel(tc, xT, w, b, gate, offs, out):
         x_scales = keep.tile([P, T], U8, name="x_scales", align_bytes=64)
         s_codes = [keep.tile([P, S], U32, name=f"s_codes{a}", align_bytes=64) for a in range(A)]
         s_scales = keep.tile([P, S], U8, name="s_scales", align_bytes=64)
-        bias = keep.tile([P, M, 2 * E], F32, name="bias")
+        bias = keep.tile([P, E, M], F32, name="bias")
         gates = keep.tile([P, S], F32, name="gates")
         windows = [keep.tile([P, T], F32, name=f"window{m}") for m in range(M)]
 
@@ -83,10 +87,16 @@ def tile_routed_moe_kernel(tc, xT, w, b, gate, offs, out):
 
         gate_row = keep.tile([P, S], F32, name="gate_row")
         ones = keep.tile([P, P], F32, name="ones")
+        b_rows = keep.tile([M, P, E], F32, name="b_rows")
+        b_laid = keep.tile([P, E, P], F32, name="b_laid")
+        identity = keep.tile([P, P], F32, name="identity")
+        nc.gpsimd.memset(b_laid[:], 0.0)
+        make_identity(nc, identity[:])
         nc.gpsimd.memset(gate_row[:], 0.0)
         nc.gpsimd.memset(x_scales[:], 0)
         nc.scalar.activation(out=ones[:], in_=gate_row[:, 0:P], func=RELU, bias=1.0, scale=1.0)
 
+        nc.sync.dma_start(b_rows[:], b.rearrange("(m p) e -> m p e", p=P))
         for a in range(A):
             nc.sync.dma_start(x_raw[a][:], x_rows[a])
             if a == 0:
@@ -94,16 +104,20 @@ def tile_routed_moe_kernel(tc, xT, w, b, gate, offs, out):
             if a == 1:
                 nc.sync.dma_start(gate_row[0:1, :], gate[0:1, :])
         for e, a in pieces:
-            if (e, a) == pieces[-1]:
+            if (e, a) in SPLIT_LOADS:
                 for lo, hi in HALVES:
                     nc.sync.dma_start(w_raw[e, a][:, :, lo:hi], w_rows[e, a, :, :, lo:hi])
             else:
                 nc.sync.dma_start(w_raw[e, a][:], w_rows[e, a])
-            if (e, a) == (0, A - 1):
-                nc.sync.dma_start(bias[:, :, 0:E], b.rearrange("(m p) e -> p m e", p=P))
 
         for m in range(M):
             nc.vector.memset(windows[m][:], 0.0)
+
+        nc.vector.tensor_copy(b_laid[0:M], b_rows[:].rearrange("m p e -> m e p"))
+        turned = psum.tile([P, E, M], F32, name="acc1")
+        for e in range(E):
+            nc.tensor.matmul(turned[:, e, :], b_laid[:, e, :], identity[:, 0:M], start=True, stop=True)
+        nc.scalar.copy(bias[:], turned[:])
 
         spread = psum.tile([P, S], F32, name="acc0")
         nc.tensor.matmul(spread[:], ones[:], gate_row[:], start=True, stop=True)
@@ -111,7 +125,7 @@ def tile_routed_moe_kernel(tc, xT, w, b, gate, offs, out):
 
         for a in range(A):
             x_grouped = xstage.tile([P, T, PACK], BF16, name="x_grouped", align_bytes=64)
-            for engine, lo, hi in X_COPIES:
+            for engine, lo, hi in X_COPIES[a]:
                 round_and_group(nc, engine, x_grouped, x_raw[a], lo, hi)
             for lo, hi in X_QUANTISE:
                 nc.vector.quantize_mx(
@@ -136,12 +150,12 @@ def tile_routed_moe_kernel(tc, xT, w, b, gate, offs, out):
             else:
                 own = keep.tile([P, C], F32, name=f"y{e}_{m}")
                 y = own[:]
-            nc.scalar.activation(out=y, in_=sums[e, m][:], func=RELU, bias=bias[:, m, e : e + 1], scale=1.0)
+            nc.scalar.activation(out=y, in_=sums[e, m][:], func=RELU, bias=bias[:, e, m : m + 1], scale=1.0)
             results.append((e, m, y))
 
         def multiply(e, a):
             slots = slice(e * C, (e + 1) * C)
-            for lo, hi in HALVES:
+            for lo, hi in (HALVES if e == 0 else W_QUANTISE[a]):
                 nc.vector.quantize_mx(
                     out=w_codes[e, a][:, lo:hi].bitcast(FP8X4),
                     scales=w_scales[e, a][:, lo:hi],

@@ -30,14 +30,14 @@ X_COPIES = [(("vector", 0, X_FIRST), ("scalar", X_FIRST, T - tail), ("vector", T
 
 HALVES = ((0, N // 2), (N // 2, N))
 HALF, QUARTER = N // 2, N // 4
-MIDDLE_CUT = 320
+MIDDLE_CUT = 352
 W_COPIES = (
     (("scalar", 0, HALF), ("vector", HALF, N)),
     (("scalar", 0, MIDDLE_CUT), ("vector", MIDDLE_CUT, N)),
-    (("scalar", 0, HALF), ("scalar", HALF, N - QUARTER), ("scalar", N - QUARTER, N)),
+    (("scalar", 0, HALF), ("scalar", HALF, N)),
 )
-W_QUANTISE = (HALVES, HALVES, ((0, HALF), (HALF, N - QUARTER), (N - QUARTER, N)))
-SPLIT_LOADS = ((E - 2, A - 1), (E - 1, A - 1))
+W_QUANTISE = (HALVES, HALVES, HALVES)
+SPLIT_LOADS = ((E - 1, A - 1),)
 W_COPIES_FIRST = (
     (("scalar", 0, N),),
     W_COPIES[1],

@@ -20,31 +20,27 @@ U16 = mybir.dt.uint16
 U8 = mybir.dt.uint8
 FP8X4 = mybir.dt.float8_e4m3fn_x4
 RELU = mybir.ActivationFunctionType.Relu
+COPY = mybir.ActivationFunctionType.Copy
 MULT = mybir.AluOpType.mult
+ADD = mybir.AluOpType.add
+MAX = mybir.AluOpType.max
 
 X_FIRST = 256
 X_QUANTISE = ((0, X_FIRST), (X_FIRST, T))
 X_TAIL = T // 2 - X_FIRST
-X_TAILS = (X_TAIL + 64, X_TAIL, X_TAIL)
-X_COPIES = [(("vector", 0, X_FIRST), ("scalar", X_FIRST, T - tail), ("vector", T - tail, T)) for tail in X_TAILS]
+X_COPIES = (("vector", 0, X_FIRST), ("scalar", X_FIRST, T - X_TAIL), ("vector", T - X_TAIL, T))
 
-HALVES = ((0, N // 2), (N // 2, N))
-HALF, QUARTER = N // 2, N // 4
-MIDDLE_CUT = 352
-W_COPIES = (
-    (("scalar", 0, HALF), ("vector", HALF, N)),
-    (("scalar", 0, MIDDLE_CUT), ("vector", MIDDLE_CUT, N)),
-    (("scalar", 0, HALF), ("scalar", HALF, N)),
-)
-W_QUANTISE = (HALVES, HALVES, HALVES)
-SPLIT_LOADS = ((E - 1, A - 1),)
-W_COPIES_FIRST = (
-    (("scalar", 0, N),),
-    W_COPIES[1],
-    (("scalar", 0, QUARTER), ("vector", QUARTER, HALF), ("scalar", HALF, N)),
-)
-LATE_BLOCK = M - 1
-LATE_PASS = 1
+HALF = N // 2
+HALVES = ((0, HALF), (HALF, N))
+BLOCKS = tuple((m * P, (m + 1) * P) for m in range(M))
+ON_VECTOR = (("vector", 0, HALF), ("vector", HALF, N))
+SHARED = (("vector", 0, HALF), ("scalar", HALF, N))
+W_COPIES = (ON_VECTOR, ON_VECTOR, SHARED)
+W_COPIES_FIRST = ((("scalar", 0, N),), SHARED, SHARED)
+LAST_COPIES = tuple(("vector", lo, hi) for lo, hi in BLOCKS)
+LAST_LOADS = HALVES
+VECTOR_SCATTERS = (3,)
+VECTOR_EMPTIES = (2, 3)
 
 
 def round_and_group(nc, engine, grouped, raw, lo, hi):
@@ -60,7 +56,7 @@ def tile_routed_moe_kernel(tc, xT, w, b, gate, offs, out):
     with ExitStack() as ctx:
         keep = ctx.enter_context(tc.tile_pool(name="keep", bufs=1))
         xstage = ctx.enter_context(tc.tile_pool(name="xstage", bufs=2))
-        wstage = ctx.enter_context(tc.tile_pool(name="wstage", bufs=4))
+        wstage = ctx.enter_context(tc.tile_pool(name="wstage", bufs=3))
         psum = ctx.enter_context(tc.psum_pool(name="psum", bufs=2))
 
         x_rows = xT.rearrange("(a p t) n -> a p t n", p=P, t=PACK)
@@ -78,12 +74,8 @@ def tile_routed_moe_kernel(tc, xT, w, b, gate, offs, out):
 
         pieces = [(e, a) for e in range(E) for a in range(A)]
         w_raw = {}
-        w_codes = {}
-        w_scales = {}
         for e, a in pieces:
             w_raw[e, a] = keep.tile([P, PACK, N], F32, name=f"w_raw{e}_{a}")
-            w_codes[e, a] = keep.tile([P, N], U32, name=f"w_codes{e}_{a}", align_bytes=64)
-            w_scales[e, a] = keep.tile([P, N], U8, name=f"w_scales{e}_{a}", align_bytes=64)
 
         gate_row = keep.tile([P, S], F32, name="gate_row")
         ones = keep.tile([P, P], F32, name="ones")
@@ -103,12 +95,10 @@ def tile_routed_moe_kernel(tc, xT, w, b, gate, offs, out):
                 nc.sync.dma_start(offsets[:], offs)
             if a == 1:
                 nc.sync.dma_start(gate_row[0:1, :], gate[0:1, :])
-        for e, a in pieces:
-            if (e, a) in SPLIT_LOADS:
-                for lo, hi in HALVES:
-                    nc.sync.dma_start(w_raw[e, a][:, :, lo:hi], w_rows[e, a, :, :, lo:hi])
-            else:
-                nc.sync.dma_start(w_raw[e, a][:], w_rows[e, a])
+        for e, a in pieces[:-1]:
+            nc.sync.dma_start(w_raw[e, a][:], w_rows[e, a])
+        for lo, hi in LAST_LOADS:
+            nc.sync.dma_start(w_raw[E - 1, A - 1][:, :, lo:hi], w_rows[E - 1, A - 1, :, :, lo:hi])
 
         for m in range(M):
             nc.vector.memset(windows[m][:], 0.0)
@@ -125,7 +115,7 @@ def tile_routed_moe_kernel(tc, xT, w, b, gate, offs, out):
 
         for a in range(A):
             x_grouped = xstage.tile([P, T, PACK], BF16, name="x_grouped", align_bytes=64)
-            for engine, lo, hi in X_COPIES[a]:
+            for engine, lo, hi in X_COPIES:
                 round_and_group(nc, engine, x_grouped, x_raw[a], lo, hi)
             for lo, hi in X_QUANTISE:
                 nc.vector.quantize_mx(
@@ -136,64 +126,66 @@ def tile_routed_moe_kernel(tc, xT, w, b, gate, offs, out):
             nc.vector.tensor_copy(s_codes[a][:], x_codes[a][:].indirect(offsets[:]))
         nc.vector.tensor_copy(s_scales[:], x_scales[:].indirect(offsets[:]))
 
-        w_grouped = {}
         sums = {}
-        results = []
+        waiting = []
 
-        def round_weights(e, a, copies):
-            for engine, lo, hi in copies:
-                round_and_group(nc, engine, w_grouped[e, a], w_raw[e, a], lo, hi)
-
-        def empty_bank(e, m):
-            if m == LATE_BLOCK and e + 1 < E:
-                y = w_raw[e + 1, LATE_PASS][:, m, 0:C]
+        def scatter(e, m, y):
+            places = offsets[:, e * C // 16 : (e + 1) * C // 16]
+            if e == E - 1 and m in VECTOR_SCATTERS:
+                nc.vector.tensor_tensor(windows[m][:].indirect(places), y, gates[:, e * C : (e + 1) * C], MULT)
             else:
-                own = keep.tile([P, C], F32, name=f"y{e}_{m}")
-                y = own[:]
-            nc.scalar.activation(out=y, in_=sums[e, m][:], func=RELU, bias=bias[:, e, m : m + 1], scale=1.0)
-            results.append((e, m, y))
+                nc.scalar.activation(windows[m][:].indirect(places), y, COPY)
+            if e == E - 1:
+                nc.sync.dma_start(out[m * P : (m + 1) * P, :], windows[m][:])
 
-        def multiply(e, a):
+        for e, a in pieces:
+            last = (e, a) == pieces[-1]
             slots = slice(e * C, (e + 1) * C)
-            for lo, hi in (HALVES if e == 0 else W_QUANTISE[a]):
+            w_grouped = wstage.tile([P, N, PACK], BF16, name="w_grouped", align_bytes=64)
+            w_codes = wstage.tile([P, N], U32, name="w_codes", align_bytes=64)
+            w_scales = wstage.tile([P, N], U8, name="w_scales", align_bytes=64)
+            copies = LAST_COPIES if last else (W_COPIES_FIRST if e == 0 else W_COPIES)[a]
+            for engine, lo, hi in copies:
+                round_and_group(nc, engine, w_grouped, w_raw[e, a], lo, hi)
+            for job in waiting:
+                scatter(*job)
+            waiting.clear()
+            for lo, hi in BLOCKS if last else HALVES:
                 nc.vector.quantize_mx(
-                    out=w_codes[e, a][:, lo:hi].bitcast(FP8X4),
-                    scales=w_scales[e, a][:, lo:hi],
-                    in_=w_grouped[e, a][:, lo:hi, :].rearrange("p n t -> p (n t)"),
+                    out=w_codes[:, lo:hi].bitcast(FP8X4),
+                    scales=w_scales[:, lo:hi],
+                    in_=w_grouped[:, lo:hi, :].rearrange("p n t -> p (n t)"),
                 )
                 for m in range(lo // P, hi // P):
                     cols = slice(m * P, (m + 1) * P)
                     if a == 0:
-                        sums[e, m] = psum.tile([P, C], F32, name=f"acc{m}")
+                        sums[m] = psum.tile([P, C], F32, name=f"acc{m}")
                     nc.tensor.matmul_mx(
-                        out=sums[e, m][:],
-                        lhsT=w_codes[e, a][:, cols].bitcast(FP8X4),
-                        lhsT_scale=w_scales[e, a][:, cols],
+                        out=sums[m][:],
+                        lhsT=w_codes[:, cols].bitcast(FP8X4),
+                        lhsT_scale=w_scales[:, cols],
                         rhs=s_codes[a][:, slots].bitcast(FP8X4),
                         rhs_scale=s_scales[PACK * a : P, slots],
                         start=(a == 0),
                         stop=(a == A - 1),
                     )
-                    if a == A - 1 and (m != LATE_BLOCK or e == E - 1):
-                        empty_bank(e, m)
-
-        for i, (e, a) in enumerate(pieces):
-            copies = (W_COPIES_FIRST if e == 0 else W_COPIES)[a]
-            w_grouped[e, a] = wstage.tile([P, N, PACK], BF16, name="w_grouped", align_bytes=64)
-            round_weights(e, a, copies[:1])
-            if i > 0:
-                multiply(*pieces[i - 1])
-            round_weights(e, a, copies[1:])
-            if e > 0 and a == LATE_PASS:
-                empty_bank(e - 1, LATE_BLOCK)
-        multiply(*pieces[-1])
-
-        for e, m, y in results:
-            nc.vector.tensor_tensor(
-                windows[m][:].indirect(offsets[:, e * C // 16 : (e + 1) * C // 16]),
-                y,
-                gates[:, e * C : (e + 1) * C],
-                MULT,
-            )
-            if e == E - 1:
-                nc.sync.dma_start(out[m * P : (m + 1) * P, :], windows[m][:])
+            if a < A - 1:
+                continue
+            y = keep.tile([P, M, C], F32, name=f"y{e}")
+            ys = [y[:, m, :] for m in range(M)]
+            for m in range(M):
+                if last and m in VECTOR_EMPTIES:
+                    nc.vector.tensor_scalar(ys[m], sums[m][:], bias[:, e, m : m + 1], 0.0, ADD, MAX)
+                else:
+                    nc.scalar.activation(out=ys[m], in_=sums[m][:], func=RELU, bias=bias[:, e, m : m + 1], scale=1.0)
+            if last:
+                for m in range(M):
+                    if m not in VECTOR_SCATTERS:
+                        nc.vector.tensor_tensor(ys[m], ys[m], gates[:, slots], MULT)
+            else:
+                for m in range(0, M, 2):
+                    pair = y[:, m : m + 2, :]
+                    nc.vector.tensor_tensor(pair, pair, gates[:, slots].unsqueeze(1).to_broadcast([P, 2, C]), MULT)
+            waiting.extend((e, m, ys[m]) for m in range(M))
+        for job in waiting:
+            scatter(*job)

@@ -34,20 +34,31 @@ HALF = N // 2
 HALVES = ((0, HALF), (HALF, N))
 BLOCKS = tuple((m * P, (m + 1) * P) for m in range(M))
 ON_VECTOR = (("vector", 0, HALF), ("vector", HALF, N))
+ON_SCALAR = (("scalar", 0, HALF), ("scalar", HALF, N))
 SHARED = (("vector", 0, HALF), ("scalar", HALF, N))
-W_COPIES = (ON_VECTOR, ON_VECTOR, SHARED)
-W_COPIES_FIRST = ((("scalar", 0, N),), SHARED, SHARED)
-LAST_COPIES = tuple(("vector", lo, hi) for lo, hi in BLOCKS)
+W_COPIES = (
+    (ON_SCALAR, ON_SCALAR, SHARED),
+    (SHARED, ON_VECTOR, ON_VECTOR),
+    (ON_VECTOR, ON_VECTOR, SHARED),
+    (ON_VECTOR, (("vector", 0, HALF), ("scalar", HALF, HALF + P), ("scalar", HALF + P, N))),
+)
+IN_ORDER = tuple((a, m) for a in range(A) for m in range(M))
+LAST_LAYOUT = IN_ORDER[:6] + ((2, 0), (2, 1), (1, 2), (2, 2), (1, 3), (2, 3))
+JOINED = (((0, 2),), ((2, 6),), ((6, 10), (10, 12)))
+APART = (((0, 2), (2, 4)), ((4, 6), (6, 8)), ((8, 10), (10, 12)))
+W_QUANTISE = (JOINED, JOINED, APART, JOINED[:2])
+LAST_QUANTISE = ((6, 7), (7, 8), (8, 10), (10, 12))
+HELD_PAIRS = ((0, 2), (0, 2), (2,))
 LAST_LOADS = HALVES
 VECTOR_SCATTERS = (3,)
 VECTOR_EMPTIES = (2, 3)
 
 
-def round_and_group(nc, engine, grouped, raw, lo, hi):
+def round_and_group(nc, engine, grouped, raw):
     copy = nc.scalar.copy if engine == "scalar" else nc.vector.tensor_copy
     copy(
-        out=grouped[:, lo:hi, :].rearrange("p (c i) (u v) -> p c u i v", i=4, v=2),
-        in_=raw[:, :, lo:hi].rearrange("p (u v) (c i) -> p c u i v", i=4, v=2),
+        out=grouped.rearrange("p (c i) (u v) -> p c u i v", i=4, v=2),
+        in_=raw.rearrange("p (u v) (c i) -> p c u i v", i=4, v=2),
     )
 
 
@@ -56,7 +67,7 @@ def tile_routed_moe_kernel(tc, xT, w, b, gate, offs, out):
     with ExitStack() as ctx:
         keep = ctx.enter_context(tc.tile_pool(name="keep", bufs=1))
         xstage = ctx.enter_context(tc.tile_pool(name="xstage", bufs=2))
-        wstage = ctx.enter_context(tc.tile_pool(name="wstage", bufs=3))
+        wstage = ctx.enter_context(tc.tile_pool(name="wstage", bufs=2))
         psum = ctx.enter_context(tc.psum_pool(name="psum", bufs=2))
 
         x_rows = xT.rearrange("(a p t) n -> a p t n", p=P, t=PACK)
@@ -116,7 +127,7 @@ def tile_routed_moe_kernel(tc, xT, w, b, gate, offs, out):
         for a in range(A):
             x_grouped = xstage.tile([P, T, PACK], BF16, name="x_grouped", align_bytes=64)
             for engine, lo, hi in X_COPIES:
-                round_and_group(nc, engine, x_grouped, x_raw[a], lo, hi)
+                round_and_group(nc, engine, x_grouped[:, lo:hi, :], x_raw[a][:, :, lo:hi])
             for lo, hi in X_QUANTISE:
                 nc.vector.quantize_mx(
                     out=x_codes[a][:, lo:hi].bitcast(FP8X4),
@@ -127,7 +138,6 @@ def tile_routed_moe_kernel(tc, xT, w, b, gate, offs, out):
         nc.vector.tensor_copy(s_scales[:], x_scales[:].indirect(offsets[:]))
 
         sums = {}
-        waiting = []
 
         def scatter(e, m, y):
             places = offsets[:, e * C // 16 : (e + 1) * C // 16]
@@ -138,54 +148,83 @@ def tile_routed_moe_kernel(tc, xT, w, b, gate, offs, out):
             if e == E - 1:
                 nc.sync.dma_start(out[m * P : (m + 1) * P, :], windows[m][:])
 
-        for e, a in pieces:
-            last = (e, a) == pieces[-1]
-            slots = slice(e * C, (e + 1) * C)
-            w_grouped = wstage.tile([P, N, PACK], BF16, name="w_grouped", align_bytes=64)
-            w_codes = wstage.tile([P, N], U32, name="w_codes", align_bytes=64)
-            w_scales = wstage.tile([P, N], U8, name="w_scales", align_bytes=64)
-            copies = LAST_COPIES if last else (W_COPIES_FIRST if e == 0 else W_COPIES)[a]
-            for engine, lo, hi in copies:
-                round_and_group(nc, engine, w_grouped, w_raw[e, a], lo, hi)
-            for job in waiting:
-                scatter(*job)
-            waiting.clear()
-            for lo, hi in BLOCKS if last else HALVES:
-                nc.vector.quantize_mx(
-                    out=w_codes[:, lo:hi].bitcast(FP8X4),
-                    scales=w_scales[:, lo:hi],
-                    in_=w_grouped[:, lo:hi, :].rearrange("p n t -> p (n t)"),
+        def round_weights(e, a, engine, lo, hi):
+            place = layout.index((a, lo // P)) * P
+            round_and_group(nc, engine, w_grouped[:, place : place + hi - lo, :], w_raw[e, a][:, :, lo:hi])
+
+        def quantise(e, first, end):
+            lo, hi = first * P, end * P
+            nc.vector.quantize_mx(
+                out=w_codes[:, lo:hi].bitcast(FP8X4),
+                scales=w_scales[:, lo:hi],
+                in_=w_grouped[:, lo:hi, :].rearrange("p n t -> p (n t)"),
+            )
+            for place in range(first, end):
+                done, m = layout[place]
+                cols = slice(place * P, (place + 1) * P)
+                if done == 0:
+                    sums[m] = psum.tile([P, C], F32, name=f"acc{m}")
+                nc.tensor.matmul_mx(
+                    out=sums[m][:],
+                    lhsT=w_codes[:, cols].bitcast(FP8X4),
+                    lhsT_scale=w_scales[:, cols],
+                    rhs=s_codes[done][:, e * C : (e + 1) * C].bitcast(FP8X4),
+                    rhs_scale=s_scales[PACK * done : P, e * C : (e + 1) * C],
+                    start=(done == 0),
+                    stop=(done == A - 1),
                 )
-                for m in range(lo // P, hi // P):
-                    cols = slice(m * P, (m + 1) * P)
-                    if a == 0:
-                        sums[m] = psum.tile([P, C], F32, name=f"acc{m}")
-                    nc.tensor.matmul_mx(
-                        out=sums[m][:],
-                        lhsT=w_codes[:, cols].bitcast(FP8X4),
-                        lhsT_scale=w_scales[:, cols],
-                        rhs=s_codes[a][:, slots].bitcast(FP8X4),
-                        rhs_scale=s_scales[PACK * a : P, slots],
-                        start=(a == 0),
-                        stop=(a == A - 1),
-                    )
-            if a < A - 1:
-                continue
-            y = keep.tile([P, M, C], F32, name=f"y{e}")
-            ys = [y[:, m, :] for m in range(M)]
-            for m in range(M):
-                if last and m in VECTOR_EMPTIES:
-                    nc.vector.tensor_scalar(ys[m], sums[m][:], bias[:, e, m : m + 1], 0.0, ADD, MAX)
-                else:
-                    nc.scalar.activation(out=ys[m], in_=sums[m][:], func=RELU, bias=bias[:, e, m : m + 1], scale=1.0)
-            if last:
-                for m in range(M):
-                    if m not in VECTOR_SCATTERS:
-                        nc.vector.tensor_tensor(ys[m], ys[m], gates[:, slots], MULT)
+
+        def empty(e, m, y):
+            if e == E - 1 and m in VECTOR_EMPTIES:
+                nc.vector.tensor_scalar(y, sums[m][:], bias[:, e, m : m + 1], 0.0, ADD, MAX)
             else:
+                nc.scalar.activation(out=y, in_=sums[m][:], func=RELU, bias=bias[:, e, m : m + 1], scale=1.0)
+
+        def gate_pair(e, gated, pair):
+            weights = gates[:, e * C : (e + 1) * C].unsqueeze(1).to_broadcast([P, 2, C])
+            nc.vector.tensor_tensor(gated, pair, weights, MULT)
+
+        for e, a in pieces[:-1]:
+            if a == 0:
+                layout = LAST_LAYOUT if e == E - 1 else IN_ORDER
+                w_grouped = wstage.tile([P, A * N, PACK], BF16, name="w_grouped", align_bytes=64)
+                w_codes = wstage.tile([P, A * N], U32, name="w_codes", align_bytes=64)
+                w_scales = wstage.tile([P, A * N], U8, name="w_scales", align_bytes=64)
+            for i, copy in enumerate(W_COPIES[e][a]):
+                round_weights(e, a, *copy)
+                if a == 0 and e > 0 and i == 0:
+                    for m in HELD_PAIRS[e - 1]:
+                        gate_pair(e - 1, w_raw[e, a][:, m : m + 2, 0:C], y[:, m : m + 2, :])
+            if a == 0 and e > 0:
+                for m in range(M):
+                    held = m - m % 2 in HELD_PAIRS[e - 1]
+                    scatter(e - 1, m, w_raw[e, a][:, m, 0:C] if held else y[:, m, :])
+            for first, end in W_QUANTISE[e][a]:
+                quantise(e, first, end)
+            if a == A - 1:
+                y = keep.tile([P, M, C], F32, name=f"y{e}")
+                for m in range(M):
+                    empty(e, m, y[:, m, :])
                 for m in range(0, M, 2):
-                    pair = y[:, m : m + 2, :]
-                    nc.vector.tensor_tensor(pair, pair, gates[:, slots].unsqueeze(1).to_broadcast([P, 2, C]), MULT)
-            waiting.extend((e, m, ys[m]) for m in range(M))
-        for job in waiting:
-            scatter(*job)
+                    if m not in HELD_PAIRS[e]:
+                        gate_pair(e, y[:, m : m + 2, :], y[:, m : m + 2, :])
+
+        e, a = pieces[-1]
+        y = keep.tile([P, M, C], F32, name=f"y{e}")
+        slots = slice(e * C, (e + 1) * C)
+        for m in range(M):
+            round_weights(e, a, "vector", *BLOCKS[m])
+            if m == 1:
+                for first in range(2):
+                    quantise(e, *LAST_QUANTISE[first])
+                    empty(e, first, y[:, first, :])
+        quantise(e, *LAST_QUANTISE[2])
+        for m in range(2):
+            nc.vector.tensor_tensor(y[:, m, :], y[:, m, :], gates[:, slots], MULT)
+            scatter(e, m, y[:, m, :])
+        quantise(e, *LAST_QUANTISE[3])
+        empty(e, 2, y[:, 2, :])
+        nc.vector.tensor_tensor(y[:, 2, :], y[:, 2, :], gates[:, slots], MULT)
+        empty(e, 3, y[:, 3, :])
+        for m in range(2, M):
+            scatter(e, m, y[:, m, :])

@@ -39,13 +39,13 @@ SHARED = (("vector", 0, HALF), ("scalar", HALF, N))
 W_COPIES = (
     (ON_SCALAR, ON_SCALAR, SHARED),
     (SHARED, ON_VECTOR, ON_VECTOR),
-    (ON_VECTOR, ON_VECTOR, SHARED),
+    (SHARED, ON_VECTOR, ON_VECTOR),
     (ON_VECTOR, (("vector", 0, HALF), ("scalar", HALF, HALF + P), ("scalar", HALF + P, N))),
 )
 IN_ORDER = tuple((a, m) for a in range(A) for m in range(M))
 LAST_LAYOUT = IN_ORDER[:6] + ((2, 0), (2, 1), (1, 2), (2, 2), (1, 3), (2, 3))
 JOINED = (((0, 2),), ((2, 6),), ((6, 10), (10, 12)))
-APART = (((0, 2), (2, 4)), ((4, 6), (6, 8)), ((8, 10), (10, 12)))
+APART = (((0, 2),), ((2, 6), (6, 8)), ((8, 10), (10, 12)))
 W_QUANTISE = (JOINED, JOINED, APART, JOINED[:2])
 LAST_QUANTISE = ((6, 7), (7, 8), (8, 10), (10, 12))
 HELD_PAIRS = ((0, 2), (0, 2), (2,))
@@ -99,10 +99,10 @@ def tile_routed_moe_kernel(tc, xT, w, b, gate, offs, out):
         nc.gpsimd.memset(x_scales[:], 0)
         nc.scalar.activation(out=ones[:], in_=gate_row[:, 0:P], func=RELU, bias=1.0, scale=1.0)
 
-        nc.sync.dma_start(b_rows[:], b.rearrange("(m p) e -> m p e", p=P))
         for a in range(A):
             nc.sync.dma_start(x_raw[a][:], x_rows[a])
             if a == 0:
+                nc.sync.dma_start(b_rows[:], b.rearrange("(m p) e -> m p e", p=P))
                 nc.sync.dma_start(offsets[:], offs)
             if a == 1:
                 nc.sync.dma_start(gate_row[0:1, :], gate[0:1, :])
@@ -218,11 +218,10 @@ def tile_routed_moe_kernel(tc, xT, w, b, gate, offs, out):
                 for first in range(2):
                     quantise(e, *LAST_QUANTISE[first])
                     empty(e, first, y[:, first, :])
-        quantise(e, *LAST_QUANTISE[2])
         for m in range(2):
             nc.vector.tensor_tensor(y[:, m, :], y[:, m, :], gates[:, slots], MULT)
             scatter(e, m, y[:, m, :])
-        quantise(e, *LAST_QUANTISE[3])
+            quantise(e, *LAST_QUANTISE[m + 2])
         empty(e, 2, y[:, 2, :])
         nc.vector.tensor_tensor(y[:, 2, :], y[:, 2, :], gates[:, slots], MULT)
         empty(e, 3, y[:, 3, :])

@@ -40,7 +40,10 @@ W_COPIES = (
     (ON_SCALAR, ON_SCALAR, SHARED),
     (SHARED, ON_VECTOR, ON_VECTOR),
     (SHARED, ON_VECTOR, ON_VECTOR),
-    (ON_VECTOR, (("vector", 0, HALF), ("scalar", HALF, HALF + P), ("scalar", HALF + P, N))),
+    (
+        (("vector", 0, P), ("vector", P, HALF), ("vector", HALF, N)),
+        (("vector", 0, HALF), ("vector", HALF, HALF + P), ("scalar", HALF + P, N)),
+    ),
 )
 IN_ORDER = tuple((a, m) for a in range(A) for m in range(M))
 LAST_LAYOUT = IN_ORDER[:6] + ((2, 0), (2, 1), (1, 2), (2, 2), (1, 3), (2, 3))
@@ -48,7 +51,7 @@ JOINED = (((0, 2),), ((2, 6),), ((6, 10), (10, 12)))
 APART = (((0, 2),), ((2, 6), (6, 8)), ((8, 10), (10, 12)))
 W_QUANTISE = (JOINED, JOINED, APART, JOINED[:2])
 LAST_QUANTISE = ((6, 7), (7, 8), (8, 10), (10, 12))
-HELD_PAIRS = ((0, 2), (0, 2), (2,))
+HELD_PAIRS = ((0, 2), (0, 2), (0, 2))
 LAST_LOADS = HALVES
 VECTOR_SCATTERS = (3,)
 VECTOR_EMPTIES = (2, 3)

@@ -221,10 +221,11 @@ def tile_routed_moe_kernel(tc, xT, w, b, gate, offs, out):
                 for first in range(2):
                     quantise(e, *LAST_QUANTISE[first])
                     empty(e, first, y[:, first, :])
+        quantise(e, *LAST_QUANTISE[2])
         for m in range(2):
             nc.vector.tensor_tensor(y[:, m, :], y[:, m, :], gates[:, slots], MULT)
             scatter(e, m, y[:, m, :])
-            quantise(e, *LAST_QUANTISE[m + 2])
+        quantise(e, *LAST_QUANTISE[3])
         empty(e, 2, y[:, 2, :])
         nc.vector.tensor_tensor(y[:, 2, :], y[:, 2, :], gates[:, slots], MULT)
         empty(e, 3, y[:, 3, :])

@@ -41,17 +41,17 @@ W_COPIES = (
     (SHARED, ON_VECTOR, ON_VECTOR),
     (SHARED, ON_VECTOR, ON_VECTOR),
     (
-        (("vector", 0, P), ("vector", P, HALF), ("vector", HALF, N)),
-        (("vector", 0, HALF), ("vector", HALF, HALF + P), ("scalar", HALF + P, N)),
+        (("vector", 0, P), ("vector", P, HALF), ("vector", HALF, HALF + P), ("scalar", HALF + P, N)),
+        (("vector", 0, HALF), ("vector", HALF, HALF + P)),
     ),
 )
 IN_ORDER = tuple((a, m) for a in range(A) for m in range(M))
 LAST_LAYOUT = IN_ORDER[:6] + ((2, 0), (2, 1), (1, 2), (2, 2), (1, 3), (2, 3))
+LOWER = ((1, 3), (2, 3))
 JOINED = (((0, 2),), ((2, 6),), ((6, 10), (10, 12)))
 APART = (((0, 2),), ((2, 6), (6, 8)), ((8, 10), (10, 12)))
-W_QUANTISE = (JOINED, JOINED, APART, JOINED[:2])
+W_QUANTISE = (JOINED, JOINED, APART, (((0, 4),), ((4, 6),)))
 LAST_QUANTISE = ((6, 7), (7, 8), (8, 10), (10, 12))
-HELD_PAIRS = ((0, 2), (0, 2), (0, 2))
 LAST_LOADS = HALVES
 VECTOR_SCATTERS = (3,)
 VECTOR_EMPTIES = (2, 3)
@@ -153,14 +153,17 @@ def tile_routed_moe_kernel(tc, xT, w, b, gate, offs, out):
 
         def round_weights(e, a, engine, lo, hi):
             place = layout.index((a, lo // P)) * P
+            if e == E - 1 and (a, lo // P) in LOWER:
+                place -= P
             round_and_group(nc, engine, w_grouped[:, place : place + hi - lo, :], w_raw[e, a][:, :, lo:hi])
 
         def quantise(e, first, end):
             lo, hi = first * P, end * P
+            lower = P if e == E - 1 and layout[first] in LOWER else 0
             nc.vector.quantize_mx(
                 out=w_codes[:, lo:hi].bitcast(FP8X4),
                 scales=w_scales[:, lo:hi],
-                in_=w_grouped[:, lo:hi, :].rearrange("p n t -> p (n t)"),
+                in_=w_grouped[:, lo - lower : hi - lower, :].rearrange("p n t -> p (n t)"),
             )
             for place in range(first, end):
                 done, m = layout[place]
@@ -196,21 +199,17 @@ def tile_routed_moe_kernel(tc, xT, w, b, gate, offs, out):
             for i, copy in enumerate(W_COPIES[e][a]):
                 round_weights(e, a, *copy)
                 if a == 0 and e > 0 and i == 0:
-                    for m in HELD_PAIRS[e - 1]:
-                        gate_pair(e - 1, w_raw[e, a][:, m : m + 2, 0:C], y[:, m : m + 2, :])
+                    gate_pair(e - 1, w_raw[e, a][:, 0:2, 0:C], y[:, 0:2, :])
             if a == 0 and e > 0:
+                gate_pair(e - 1, w_raw[e, a][:, 2:4, 0:C], y[:, 2:4, :])
                 for m in range(M):
-                    held = m - m % 2 in HELD_PAIRS[e - 1]
-                    scatter(e - 1, m, w_raw[e, a][:, m, 0:C] if held else y[:, m, :])
+                    scatter(e - 1, m, w_raw[e, a][:, m, 0:C])
             for first, end in W_QUANTISE[e][a]:
                 quantise(e, first, end)
             if a == A - 1:
                 y = keep.tile([P, M, C], F32, name=f"y{e}")
                 for m in range(M):
                     empty(e, m, y[:, m, :])
-                for m in range(0, M, 2):
-                    if m not in HELD_PAIRS[e]:
-                        gate_pair(e, y[:, m : m + 2, :], y[:, m : m + 2, :])
 
         e, a = pieces[-1]
         y = keep.tile([P, M, C], F32, name=f"y{e}")
@@ -225,8 +224,9 @@ def tile_routed_moe_kernel(tc, xT, w, b, gate, offs, out):
         for m in range(2):
             nc.vector.tensor_tensor(y[:, m, :], y[:, m, :], gates[:, slots], MULT)
             scatter(e, m, y[:, m, :])
-        quantise(e, *LAST_QUANTISE[3])
+        round_weights(e, a - 1, "vector", *BLOCKS[3])
         empty(e, 2, y[:, 2, :])
+        quantise(e, *LAST_QUANTISE[3])
         nc.vector.tensor_tensor(y[:, 2, :], y[:, 2, :], gates[:, slots], MULT)
         empty(e, 3, y[:, 3, :])
         for m in range(2, M):

@@ -52,7 +52,7 @@ JOINED = (((0, 2),), ((2, 6),), ((6, 10), (10, 12)))
 APART = (((0, 2),), ((2, 6), (6, 8)), ((8, 10), (10, 12)))
 W_QUANTISE = (JOINED, JOINED, APART, (((0, 4),), ((4, 6),)))
 LAST_QUANTISE = ((6, 7), (7, 8), (8, 10), (10, 12))
-LAST_LOADS = HALVES
+LAST_LOADS = (HALVES[0],) + BLOCKS[2:]
 VECTOR_SCATTERS = (3,)
 VECTOR_EMPTIES = (2, 3)
 
@@ -154,12 +154,12 @@ def tile_routed_moe_kernel(tc, xT, w, b, gate, offs, out):
         def round_weights(e, a, engine, lo, hi):
             place = layout.index((a, lo // P)) * P
             if e == E - 1 and (a, lo // P) in LOWER:
-                place -= P
+                place -= 3 * P
             round_and_group(nc, engine, w_grouped[:, place : place + hi - lo, :], w_raw[e, a][:, :, lo:hi])
 
         def quantise(e, first, end):
             lo, hi = first * P, end * P
-            lower = P if e == E - 1 and layout[first] in LOWER else 0
+            lower = 3 * P if e == E - 1 and layout[first] in LOWER else 0
             nc.vector.quantize_mx(
                 out=w_codes[:, lo:hi].bitcast(FP8X4),
                 scales=w_scales[:, lo:hi],
@@ -214,19 +214,21 @@ def tile_routed_moe_kernel(tc, xT, w, b, gate, offs, out):
         e, a = pieces[-1]
         y = keep.tile([P, M, C], F32, name=f"y{e}")
         slots = slice(e * C, (e + 1) * C)
-        for m in range(M):
+        for m in range(2):
             round_weights(e, a, "vector", *BLOCKS[m])
-            if m == 1:
-                for first in range(2):
-                    quantise(e, *LAST_QUANTISE[first])
-                    empty(e, first, y[:, first, :])
+        for m in range(2):
+            quantise(e, *LAST_QUANTISE[m])
+            empty(e, m, y[:, m, :])
+        round_weights(e, a, "vector", *BLOCKS[2])
+        round_weights(e, a - 1, "vector", *BLOCKS[3])
         quantise(e, *LAST_QUANTISE[2])
         for m in range(2):
             nc.vector.tensor_tensor(y[:, m, :], y[:, m, :], gates[:, slots], MULT)
             scatter(e, m, y[:, m, :])
-        round_weights(e, a - 1, "vector", *BLOCKS[3])
-        empty(e, 2, y[:, 2, :])
+            if m == 0:
+                round_weights(e, a, "vector", *BLOCKS[3])
         quantise(e, *LAST_QUANTISE[3])
+        empty(e, 2, y[:, 2, :])
         nc.vector.tensor_tensor(y[:, 2, :], y[:, 2, :], gates[:, slots], MULT)
         empty(e, 3, y[:, 3, :])
         for m in range(2, M):

@@ -36,10 +36,11 @@ BLOCKS = tuple((m * P, (m + 1) * P) for m in range(M))
 ON_VECTOR = (("vector", 0, HALF), ("vector", HALF, N))
 ON_SCALAR = (("scalar", 0, HALF), ("scalar", HALF, N))
 SHARED = (("vector", 0, HALF), ("scalar", HALF, N))
+LAST_BAND = (("vector", 0, HALF), ("vector", HALF, HALF + P), ("scalar", HALF + P, N))
 W_COPIES = (
     (ON_SCALAR, ON_SCALAR, SHARED),
     (SHARED, ON_VECTOR, ON_VECTOR),
-    (SHARED, ON_VECTOR, ON_VECTOR),
+    (LAST_BAND, ON_VECTOR, LAST_BAND),
     (
         (("vector", 0, P), ("vector", P, HALF), ("vector", HALF, HALF + P), ("scalar", HALF + P, N)),
         (("vector", 0, HALF), ("vector", HALF, HALF + P)),

@@ -42,20 +42,19 @@ W_COPIES = (
     (SHARED, ON_VECTOR, ON_VECTOR),
     (LAST_BAND, ON_VECTOR, LAST_BAND),
     (
-        (("vector", 0, P), ("vector", P, HALF), ("vector", HALF, HALF + P), ("scalar", HALF + P, N)),
-        (("vector", 0, HALF), ("vector", HALF, HALF + P)),
+        (("vector", 0, P), ("vector", P, HALF + P), ("scalar", HALF + P, N)),
+        (("vector", 0, HALF),),
     ),
 )
 IN_ORDER = tuple((a, m) for a in range(A) for m in range(M))
-LAST_LAYOUT = IN_ORDER[:6] + ((2, 0), (2, 1), (1, 2), (2, 2), (1, 3), (2, 3))
-LOWER = ((1, 3), (2, 3))
+LAST_LAYOUT = IN_ORDER[:6] + ((2, 0), (2, 1), (2, 2), (1, 2), (1, 3), (2, 3))
 JOINED = (((0, 2),), ((2, 6),), ((6, 10), (10, 12)))
 APART = (((0, 2),), ((2, 6), (6, 8)), ((8, 10), (10, 12)))
-W_QUANTISE = (JOINED, JOINED, APART, (((0, 4),), ((4, 6),)))
-LAST_QUANTISE = ((6, 7), (7, 8), (8, 10), (10, 12))
-LAST_LOADS = (HALVES[0],) + BLOCKS[2:]
+W_QUANTISE = (JOINED, JOINED, APART, (((0, 4),), ()))
+LAST_QUANTISE = ((4, 7), (7, 8), (8, 10), (10, 12))
+LAST_LOADS = ((1, HALVES[0]), (2, HALVES[0]), (1, HALVES[1]), (2, HALVES[1]))
 VECTOR_SCATTERS = (3,)
-VECTOR_EMPTIES = (2, 3)
+VECTOR_EMPTIES = (0, 2)
 
 
 def round_and_group(nc, engine, grouped, raw):
@@ -110,10 +109,10 @@ def tile_routed_moe_kernel(tc, xT, w, b, gate, offs, out):
                 nc.sync.dma_start(offsets[:], offs)
             if a == 1:
                 nc.sync.dma_start(gate_row[0:1, :], gate[0:1, :])
-        for e, a in pieces[:-1]:
+        for e, a in pieces[:-2]:
             nc.sync.dma_start(w_raw[e, a][:], w_rows[e, a])
-        for lo, hi in LAST_LOADS:
-            nc.sync.dma_start(w_raw[E - 1, A - 1][:, :, lo:hi], w_rows[E - 1, A - 1, :, :, lo:hi])
+        for a, (lo, hi) in LAST_LOADS:
+            nc.sync.dma_start(w_raw[E - 1, a][:, :, lo:hi], w_rows[E - 1, a, :, :, lo:hi])
 
         for m in range(M):
             nc.vector.memset(windows[m][:], 0.0)
@@ -154,20 +153,17 @@ def tile_routed_moe_kernel(tc, xT, w, b, gate, offs, out):
 
         def round_weights(e, a, engine, lo, hi):
             place = layout.index((a, lo // P)) * P
-            if e == E - 1 and (a, lo // P) in LOWER:
-                place -= 3 * P
             round_and_group(nc, engine, w_grouped[:, place : place + hi - lo, :], w_raw[e, a][:, :, lo:hi])
 
         def quantise(e, first, end):
             lo, hi = first * P, end * P
-            lower = 3 * P if e == E - 1 and layout[first] in LOWER else 0
             nc.vector.quantize_mx(
                 out=w_codes[:, lo:hi].bitcast(FP8X4),
                 scales=w_scales[:, lo:hi],
-                in_=w_grouped[:, lo - lower : hi - lower, :].rearrange("p n t -> p (n t)"),
+                in_=w_grouped[:, lo:hi, :].rearrange("p n t -> p (n t)"),
             )
-            for place in range(first, end):
-                done, m = layout[place]
+            for m, done in sorted((m, done) for done, m in layout[first:end]):
+                place = layout.index((done, m))
                 cols = slice(place * P, (place + 1) * P)
                 if done == 0:
                     sums[m] = psum.tile([P, C], F32, name=f"acc{m}")
@@ -219,15 +215,16 @@ def tile_routed_moe_kernel(tc, xT, w, b, gate, offs, out):
             round_weights(e, a, "vector", *BLOCKS[m])
         for m in range(2):
             quantise(e, *LAST_QUANTISE[m])
-            empty(e, m, y[:, m, :])
-        round_weights(e, a, "vector", *BLOCKS[2])
-        round_weights(e, a - 1, "vector", *BLOCKS[3])
-        quantise(e, *LAST_QUANTISE[2])
+        round_weights(e, a - 1, "vector", *HALVES[1])
         for m in range(2):
-            nc.vector.tensor_tensor(y[:, m, :], y[:, m, :], gates[:, slots], MULT)
-            scatter(e, m, y[:, m, :])
-            if m == 0:
-                round_weights(e, a, "vector", *BLOCKS[3])
+            empty(e, m, y[:, m, :])
+        for m in range(2):
+            round_weights(e, a, "vector", *BLOCKS[2 + m])
+            if m == 1:
+                quantise(e, *LAST_QUANTISE[2])
+            gated = w_raw[e, a][:, 0, slice(*BLOCKS[2 + m])] if m else y[:, 0, :]
+            nc.vector.tensor_tensor(gated, y[:, m, :], gates[:, slots], MULT)
+            scatter(e, m, gated)
         quantise(e, *LAST_QUANTISE[3])
         empty(e, 2, y[:, 2, :])
         nc.vector.tensor_tensor(y[:, 2, :], y[:, 2, :], gates[:, slots], MULT)

@@ -31,30 +31,9 @@ X_TAIL = T // 2 - X_FIRST
 X_COPIES = (("vector", 0, X_FIRST), ("scalar", X_FIRST, T - X_TAIL), ("vector", T - X_TAIL, T))
 
 HALF = N // 2
-HALVES = ((0, HALF), (HALF, N))
-BLOCKS = tuple((m * P, (m + 1) * P) for m in range(M))
-ON_VECTOR = (("vector", 0, HALF), ("vector", HALF, N))
-ON_SCALAR = (("scalar", 0, HALF), ("scalar", HALF, N))
-SHARED = (("vector", 0, HALF), ("scalar", HALF, N))
-LAST_BAND = (("vector", 0, HALF), ("vector", HALF, HALF + P), ("scalar", HALF + P, N))
-W_COPIES = (
-    (ON_SCALAR, ON_SCALAR, SHARED),
-    (SHARED, ON_VECTOR, ON_VECTOR),
-    (LAST_BAND, ON_VECTOR, LAST_BAND),
-    (
-        (("vector", 0, P), ("vector", P, HALF + P), ("scalar", HALF + P, N)),
-        (("vector", 0, HALF),),
-    ),
-)
+LAST = E - 1
 IN_ORDER = tuple((a, m) for a in range(A) for m in range(M))
-LAST_LAYOUT = IN_ORDER[:6] + ((2, 0), (2, 1), (2, 2), (1, 2), (1, 3), (2, 3))
-JOINED = (((0, 2),), ((2, 6),), ((6, 10), (10, 12)))
-APART = (((0, 2),), ((2, 6), (6, 8)), ((8, 10), (10, 12)))
-W_QUANTISE = (JOINED, JOINED, APART, (((0, 4),), ()))
-LAST_QUANTISE = ((4, 7), (7, 8), (8, 10), (10, 12))
-LAST_LOADS = ((1, HALVES[0]), (2, HALVES[0]), (1, HALVES[1]), (2, HALVES[1]))
-VECTOR_SCATTERS = (3,)
-VECTOR_EMPTIES = (0, 2)
+LAST_LAYOUT = IN_ORDER[:6] + ((2, 0), (2, 1), (1, 2), (2, 2), (1, 3), (2, 3))
 
 
 def round_and_group(nc, engine, grouped, raw):
@@ -63,6 +42,10 @@ def round_and_group(nc, engine, grouped, raw):
         out=grouped.rearrange("p (c i) (u v) -> p c u i v", i=4, v=2),
         in_=raw.rearrange("p (u v) (c i) -> p c u i v", i=4, v=2),
     )
+
+
+def band(first, end=None):
+    return slice(first * P, (first + 1 if end is None else end) * P)
 
 
 def tile_routed_moe_kernel(tc, xT, w, b, gate, offs, out):
@@ -85,11 +68,8 @@ def tile_routed_moe_kernel(tc, xT, w, b, gate, offs, out):
         bias = keep.tile([P, E, M], F32, name="bias")
         gates = keep.tile([P, S], F32, name="gates")
         windows = [keep.tile([P, T], F32, name=f"window{m}") for m in range(M)]
-
-        pieces = [(e, a) for e in range(E) for a in range(A)]
-        w_raw = {}
-        for e, a in pieces:
-            w_raw[e, a] = keep.tile([P, PACK, N], F32, name=f"w_raw{e}_{a}")
+        w_raw = {(e, a): keep.tile([P, PACK, N], F32, name=f"w_raw{e}_{a}") for e in range(E) for a in range(A)}
+        y = [keep.tile([P, M, C], F32, name=f"y{e}") for e in range(E)]
 
         gate_row = keep.tile([P, S], F32, name="gate_row")
         ones = keep.tile([P, P], F32, name="ones")
@@ -109,10 +89,13 @@ def tile_routed_moe_kernel(tc, xT, w, b, gate, offs, out):
                 nc.sync.dma_start(offsets[:], offs)
             if a == 1:
                 nc.sync.dma_start(gate_row[0:1, :], gate[0:1, :])
-        for e, a in pieces[:-2]:
-            nc.sync.dma_start(w_raw[e, a][:], w_rows[e, a])
-        for a, (lo, hi) in LAST_LOADS:
-            nc.sync.dma_start(w_raw[E - 1, a][:, :, lo:hi], w_rows[E - 1, a, :, :, lo:hi])
+        for e in range(LAST):
+            for a in range(A):
+                nc.sync.dma_start(w_raw[e, a][:], w_rows[e, a])
+        nc.sync.dma_start(w_raw[LAST, 0][:], w_rows[LAST, 0])
+        for cols in (band(0, 2), band(2, 4)):
+            for a in (1, 2):
+                nc.sync.dma_start(w_raw[LAST, a][:, :, cols], w_rows[LAST, a, :, :, cols])
 
         for m in range(M):
             nc.vector.memset(windows[m][:], 0.0)
@@ -140,94 +123,130 @@ def tile_routed_moe_kernel(tc, xT, w, b, gate, offs, out):
             nc.vector.tensor_copy(s_codes[a][:], x_codes[a][:].indirect(offsets[:]))
         nc.vector.tensor_copy(s_scales[:], x_scales[:].indirect(offsets[:]))
 
+        stage = {}
         sums = {}
 
-        def scatter(e, m, y):
-            places = offsets[:, e * C // 16 : (e + 1) * C // 16]
-            if e == E - 1 and m in VECTOR_SCATTERS:
-                nc.vector.tensor_tensor(windows[m][:].indirect(places), y, gates[:, e * C : (e + 1) * C], MULT)
-            else:
-                nc.scalar.activation(windows[m][:].indirect(places), y, COPY)
-            if e == E - 1:
-                nc.sync.dma_start(out[m * P : (m + 1) * P, :], windows[m][:])
-
-        def round_weights(e, a, engine, lo, hi):
-            place = layout.index((a, lo // P)) * P
-            round_and_group(nc, engine, w_grouped[:, place : place + hi - lo, :], w_raw[e, a][:, :, lo:hi])
-
-        def quantise(e, first, end):
-            lo, hi = first * P, end * P
-            nc.vector.quantize_mx(
-                out=w_codes[:, lo:hi].bitcast(FP8X4),
-                scales=w_scales[:, lo:hi],
-                in_=w_grouped[:, lo:hi, :].rearrange("p n t -> p (n t)"),
+        def open_expert(e):
+            stage[e] = (
+                LAST_LAYOUT if e == LAST else IN_ORDER,
+                wstage.tile([P, A * N, PACK], BF16, name="w_grouped", align_bytes=64),
+                wstage.tile([P, A * N], U32, name="w_codes", align_bytes=64),
+                wstage.tile([P, A * N], U8, name="w_scales", align_bytes=64),
             )
-            for m, done in sorted((m, done) for done, m in layout[first:end]):
-                place = layout.index((done, m))
-                cols = slice(place * P, (place + 1) * P)
+
+        def rounded(engine, e, a, first, end=None):
+            layout, grouped = stage[e][:2]
+            cols = band(first, end)
+            place = layout.index((a, first)) * P
+            round_and_group(nc, engine, grouped[:, place : place + cols.stop - cols.start, :], w_raw[e, a][:, :, cols])
+
+        def multiply(e, a, m, count=1):
+            layout, grouped, codes, scales = stage[e]
+            first = layout.index((a, m))
+            places = band(first, first + count)
+            nc.vector.quantize_mx(
+                out=codes[:, places].bitcast(FP8X4),
+                scales=scales[:, places],
+                in_=grouped[:, places, :].rearrange("p n t -> p (n t)"),
+            )
+            for place in range(first, first + count):
+                done, which = layout[place]
                 if done == 0:
-                    sums[m] = psum.tile([P, C], F32, name=f"acc{m}")
+                    sums[e, which] = psum.tile([P, C], F32, name=f"acc{which}")
                 nc.tensor.matmul_mx(
-                    out=sums[m][:],
-                    lhsT=w_codes[:, cols].bitcast(FP8X4),
-                    lhsT_scale=w_scales[:, cols],
-                    rhs=s_codes[done][:, e * C : (e + 1) * C].bitcast(FP8X4),
-                    rhs_scale=s_scales[PACK * done : P, e * C : (e + 1) * C],
+                    out=sums[e, which][:],
+                    lhsT=codes[:, band(place)].bitcast(FP8X4),
+                    lhsT_scale=scales[:, band(place)],
+                    rhs=s_codes[done][:, band(e)].bitcast(FP8X4),
+                    rhs_scale=s_scales[PACK * done : P, band(e)],
                     start=(done == 0),
                     stop=(done == A - 1),
                 )
 
-        def empty(e, m, y):
-            if e == E - 1 and m in VECTOR_EMPTIES:
-                nc.vector.tensor_scalar(y, sums[m][:], bias[:, e, m : m + 1], 0.0, ADD, MAX)
+        def empty(engine, e, m, into):
+            if engine == "vector":
+                nc.vector.tensor_scalar(into, sums[e, m][:], bias[:, e, m : m + 1], 0.0, ADD, MAX)
             else:
-                nc.scalar.activation(out=y, in_=sums[m][:], func=RELU, bias=bias[:, e, m : m + 1], scale=1.0)
+                nc.scalar.activation(out=into, in_=sums[e, m][:], func=RELU, bias=bias[:, e, m : m + 1], scale=1.0)
 
-        def gate_pair(e, gated, pair):
-            weights = gates[:, e * C : (e + 1) * C].unsqueeze(1).to_broadcast([P, 2, C])
-            nc.vector.tensor_tensor(gated, pair, weights, MULT)
+        def gated(e, into, values):
+            weights = gates[:, band(e)].unsqueeze(1).to_broadcast(list(values.shape))
+            nc.vector.tensor_tensor(into, values, weights, MULT)
 
-        for e, a in pieces[:-1]:
-            if a == 0:
-                layout = LAST_LAYOUT if e == E - 1 else IN_ORDER
-                w_grouped = wstage.tile([P, A * N, PACK], BF16, name="w_grouped", align_bytes=64)
-                w_codes = wstage.tile([P, A * N], U32, name="w_codes", align_bytes=64)
-                w_scales = wstage.tile([P, A * N], U8, name="w_scales", align_bytes=64)
-            for i, copy in enumerate(W_COPIES[e][a]):
-                round_weights(e, a, *copy)
-                if a == 0 and e > 0 and i == 0:
-                    gate_pair(e - 1, w_raw[e, a][:, 0:2, 0:C], y[:, 0:2, :])
-            if a == 0 and e > 0:
-                gate_pair(e - 1, w_raw[e, a][:, 2:4, 0:C], y[:, 2:4, :])
-                for m in range(M):
-                    scatter(e - 1, m, w_raw[e, a][:, m, 0:C])
-            for first, end in W_QUANTISE[e][a]:
-                quantise(e, first, end)
-            if a == A - 1:
-                y = keep.tile([P, M, C], F32, name=f"y{e}")
-                for m in range(M):
-                    empty(e, m, y[:, m, :])
+        def scatter(engine, e, m, values):
+            window = windows[m][:].indirect(offsets[:, e * C // 16 : (e + 1) * C // 16])
+            if engine == "vector":
+                nc.vector.tensor_tensor(window, values, gates[:, band(e)], MULT)
+            else:
+                nc.scalar.activation(window, values, COPY)
+            if e == LAST:
+                nc.sync.dma_start(out[band(m), :], windows[m][:])
 
-        e, a = pieces[-1]
-        y = keep.tile([P, M, C], F32, name=f"y{e}")
-        slots = slice(e * C, (e + 1) * C)
+        def last_pass(e):
+            for m in range(M):
+                rounded("vector" if m < 2 else "scalar", e, 2, m)
+            for m in range(M):
+                multiply(e, 2, m)
+                empty("scalar", e, m, y[e][:, m, :])
+            gated(e, y[e][:, 0:1, :], y[e][:, 0:1, :])
+            scatter("scalar", e, 0, y[e][:, 0, :])
+
+        def first_bands(e):
+            rounded("vector", e, 0, 0)
+            held = w_raw[e, 0][:, 1:M, band(0)]
+            gated(e - 1, held, y[e - 1][:, 1:M, :])
+            rounded("vector", e, 0, 1)
+            return held
+
+        open_expert(0)
+        rounded("scalar", 0, 0, 0, 2)
+        rounded("scalar", 0, 0, 2, 4)
+        multiply(0, 0, 0, 4)
+        rounded("scalar", 0, 1, 0, 2)
+        rounded("vector", 0, 1, 2, 4)
+        multiply(0, 1, 0, 2)
+        multiply(0, 1, 2, 2)
+        last_pass(0)
+
+        for e in range(1, LAST):
+            open_expert(e)
+            held = first_bands(e)
+            for m in range(1, M):
+                scatter("scalar", e - 1, m, held[:, m - 1, :])
+            rounded("vector", e, 0, 2, 4)
+            multiply(e, 0, 0, 2)
+            rounded("vector", e, 1, 0, 2)
+            rounded("vector", e, 1, 2, 4)
+            multiply(e, 0, 2, 4)
+            multiply(e, 1, 2, 2)
+            last_pass(e)
+
+        e = LAST
+        open_expert(e)
+        held = first_bands(e)
+        rounded("scalar", e, 0, 2, 4)
+        for m in range(1, M):
+            scatter("scalar", e - 1, m, held[:, m - 1, :])
+        multiply(e, 0, 0, 2)
+        rounded("vector", e, 1, 0, 2)
+        multiply(e, 0, 2, 2)
+        multiply(e, 1, 0, 2)
         for m in range(2):
-            round_weights(e, a, "vector", *BLOCKS[m])
+            rounded("vector", e, 2, m)
         for m in range(2):
-            quantise(e, *LAST_QUANTISE[m])
-        round_weights(e, a - 1, "vector", *HALVES[1])
-        for m in range(2):
-            empty(e, m, y[:, m, :])
-        for m in range(2):
-            round_weights(e, a, "vector", *BLOCKS[2 + m])
-            if m == 1:
-                quantise(e, *LAST_QUANTISE[2])
-            gated = w_raw[e, a][:, 0, slice(*BLOCKS[2 + m])] if m else y[:, 0, :]
-            nc.vector.tensor_tensor(gated, y[:, m, :], gates[:, slots], MULT)
-            scatter(e, m, gated)
-        quantise(e, *LAST_QUANTISE[3])
-        empty(e, 2, y[:, 2, :])
-        nc.vector.tensor_tensor(y[:, 2, :], y[:, 2, :], gates[:, slots], MULT)
-        empty(e, 3, y[:, 3, :])
-        for m in range(2, M):
-            scatter(e, m, y[:, m, :])
+            multiply(e, 2, m)
+        rounded("vector", e, 1, 2)
+        empty("vector", e, 0, y[e][:, 0, :])
+        rounded("vector", e, 1, 3)
+        gated(e, y[e][:, 0:1, :], y[e][:, 0:1, :])
+        spent = w_raw[e, 1][:, 0, band(3)]
+        empty("scalar", e, 1, spent)
+        scatter("scalar", e, 0, y[e][:, 0, :])
+        for m in (2, 3):
+            rounded("vector", e, 2, m)
+        for m in (2, 3):
+            multiply(e, 1, m, 2)
+        scatter("vector", e, 1, spent)
+        for m in (2, 3):
+            empty("scalar", e, m, y[e][:, m, :])
+            scatter("vector", e, m, y[e][:, m, :])

@@ -33,7 +33,7 @@ X_COPIES = (("vector", 0, X_FIRST), ("scalar", X_FIRST, T - X_TAIL), ("vector", 
 HALF = N // 2
 LAST = E - 1
 IN_ORDER = tuple((a, m) for a in range(A) for m in range(M))
-LAST_LAYOUT = IN_ORDER[:6] + ((2, 0), (2, 1), (1, 2), (2, 2), (1, 3), (2, 3))
+LAST_LAYOUT = ((0, 0), (0, 1), (1, 0), (1, 1), (2, 0), (2, 1), (0, 2), (0, 3), (1, 2), (2, 2), (1, 3), (2, 3))
 
 
 def round_and_group(nc, engine, grouped, raw):
@@ -182,71 +182,67 @@ def tile_routed_moe_kernel(tc, xT, w, b, gate, offs, out):
             if e == LAST:
                 nc.sync.dma_start(out[band(m), :], windows[m][:])
 
-        def last_pass(e):
-            for m in range(M):
-                rounded("vector" if m < 2 else "scalar", e, 2, m)
-            for m in range(M):
-                multiply(e, 2, m)
-                empty("scalar", e, m, y[e][:, m, :])
-            gated(e, y[e][:, 0:1, :], y[e][:, 0:1, :])
-            scatter("scalar", e, 0, y[e][:, 0, :])
-
-        def first_bands(e):
-            rounded("vector", e, 0, 0)
-            held = w_raw[e, 0][:, 1:M, band(0)]
-            gated(e - 1, held, y[e - 1][:, 1:M, :])
-            rounded("vector", e, 0, 1)
-            return held
+        def first_pass(e, bands):
+            rounded("vector", e, 0, 0, 2)
+            multiply(e, 0, 0, 2)
+            rounded("scalar", e, 0, 2, 4)
+            held = w_raw[e, 0][:, :, band(0)]
+            for first, end in bands:
+                gated(e - 1, held[:, first:end, :], y[e - 1][:, first:end, :])
+                for m in range(first, end):
+                    scatter("scalar", e - 1, m, held[:, m, :])
 
         open_expert(0)
-        rounded("scalar", 0, 0, 0, 2)
-        rounded("scalar", 0, 0, 2, 4)
-        multiply(0, 0, 0, 4)
-        rounded("scalar", 0, 1, 0, 2)
-        rounded("vector", 0, 1, 2, 4)
-        multiply(0, 1, 0, 2)
-        multiply(0, 1, 2, 2)
-        last_pass(0)
+        for a in range(2):
+            rounded("scalar", 0, a, 0, 2)
+            rounded("scalar", 0, a, 2, 4)
+        multiply(0, 0, 0, 2)
+        multiply(0, 0, 2, 4)
+        rounded("vector", 0, 2, 0, 2)
+        rounded("scalar", 0, 2, 2, 4)
+        multiply(0, 1, 2, 4)
+        multiply(0, 2, 2, 2)
+        for m in range(M):
+            empty("scalar", 0, m, y[0][:, m, :])
 
         for e in range(1, LAST):
             open_expert(e)
-            held = first_bands(e)
-            for m in range(1, M):
-                scatter("scalar", e - 1, m, held[:, m - 1, :])
-            rounded("vector", e, 0, 2, 4)
-            multiply(e, 0, 0, 2)
+            first_pass(e, ((0, 2), (2, 4)))
             rounded("vector", e, 1, 0, 2)
             rounded("vector", e, 1, 2, 4)
             multiply(e, 0, 2, 4)
             multiply(e, 1, 2, 2)
-            last_pass(e)
+            rounded("vector", e, 2, 0, 2)
+            rounded("vector", e, 2, 2, 4)
+            multiply(e, 2, 0, 2)
+            multiply(e, 2, 2, 2)
+            for m in range(M):
+                empty("scalar", e, m, y[e][:, m, :])
 
         e = LAST
         open_expert(e)
-        held = first_bands(e)
-        rounded("scalar", e, 0, 2, 4)
-        for m in range(1, M):
-            scatter("scalar", e - 1, m, held[:, m - 1, :])
-        multiply(e, 0, 0, 2)
+        first_pass(e, ((0, 3),))
         rounded("vector", e, 1, 0, 2)
-        multiply(e, 0, 2, 2)
-        multiply(e, 1, 0, 2)
         for m in range(2):
             rounded("vector", e, 2, m)
-        for m in range(2):
-            multiply(e, 2, m)
+        multiply(e, 1, 0, 3)
+        multiply(e, 2, 1, 3)
         rounded("vector", e, 1, 2)
+        rounded("scalar", e, 1, 3)
         empty("vector", e, 0, y[e][:, 0, :])
-        rounded("vector", e, 1, 3)
+        rounded("vector", e, 2, 2)
         gated(e, y[e][:, 0:1, :], y[e][:, 0:1, :])
-        spent = w_raw[e, 1][:, 0, band(3)]
+        spent = w_raw[e, 2][:, 0, band(2)]
         empty("scalar", e, 1, spent)
         scatter("scalar", e, 0, y[e][:, 0, :])
-        for m in (2, 3):
-            rounded("vector", e, 2, m)
+        rounded("vector", e, 2, 3)
         for m in (2, 3):
             multiply(e, 1, m, 2)
+        late = w_raw[e, 2][:, 0:1, band(3)]
+        gated(e - 1, late, y[e - 1][:, 3:4, :])
         scatter("vector", e, 1, spent)
         for m in (2, 3):
             empty("scalar", e, m, y[e][:, m, :])
+        scatter("scalar", e - 1, 3, late[:, 0, :])
+        for m in (2, 3):
             scatter("vector", e, m, y[e][:, m, :])

@@ -33,7 +33,7 @@ X_COPIES = (("vector", 0, X_FIRST), ("scalar", X_FIRST, T - X_TAIL), ("vector", 
 HALF = N // 2
 LAST = E - 1
 IN_ORDER = tuple((a, m) for a in range(A) for m in range(M))
-LAST_LAYOUT = ((0, 0), (0, 1), (1, 0), (1, 1), (2, 0), (2, 1), (0, 2), (0, 3), (1, 2), (2, 2), (1, 3), (2, 3))
+LAST_LAYOUT = ((0, 0), (0, 1), (1, 0), (1, 1), (2, 0), (2, 1), (0, 2), (0, 3), (2, 2), (1, 2), (1, 3), (2, 3))
 
 
 def round_and_group(nc, engine, grouped, raw):
@@ -149,8 +149,8 @@ def tile_routed_moe_kernel(tc, xT, w, b, gate, offs, out):
                 scales=scales[:, places],
                 in_=grouped[:, places, :].rearrange("p n t -> p (n t)"),
             )
-            for place in range(first, first + count):
-                done, which = layout[place]
+            for done, which in sorted(layout[first : first + count]):
+                place = layout.index((done, which))
                 if done == 0:
                     sums[e, which] = psum.tile([P, C], F32, name=f"acc{which}")
                 nc.tensor.matmul_mx(
@@ -221,23 +221,29 @@ def tile_routed_moe_kernel(tc, xT, w, b, gate, offs, out):
 
         e = LAST
         open_expert(e)
-        first_pass(e, ((0, 3),))
+        rounded("vector", e, 0, 0, 2)
+        rounded("vector", e, 0, 2)
+        rounded("scalar", e, 0, 3)
+        held = w_raw[e, 0][:, :, band(0)]
+        gated(e - 1, held[:, 0:3, :], y[e - 1][:, 0:3, :])
+        for m in range(3):
+            scatter("scalar", e - 1, m, held[:, m, :])
+        multiply(e, 0, 0, 2)
         rounded("vector", e, 1, 0, 2)
         for m in range(2):
             rounded("vector", e, 2, m)
         multiply(e, 1, 0, 3)
         multiply(e, 2, 1, 3)
-        rounded("vector", e, 1, 2)
-        rounded("scalar", e, 1, 3)
-        empty("vector", e, 0, y[e][:, 0, :])
-        rounded("vector", e, 2, 2)
+        empty("scalar", e, 0, y[e][:, 0, :])
+        rounded("vector", e, 1, 2, 4)
         gated(e, y[e][:, 0:1, :], y[e][:, 0:1, :])
-        spent = w_raw[e, 2][:, 0, band(2)]
+        spent = w_raw[e, 1][:, 0, band(3)]
         empty("scalar", e, 1, spent)
         scatter("scalar", e, 0, y[e][:, 0, :])
+        rounded("vector", e, 2, 2)
         rounded("vector", e, 2, 3)
-        for m in (2, 3):
-            multiply(e, 1, m, 2)
+        multiply(e, 2, 2, 2)
+        multiply(e, 1, 3, 2)
         late = w_raw[e, 2][:, 0:1, band(3)]
         gated(e - 1, late, y[e - 1][:, 3:4, :])
         scatter("vector", e, 1, spent)

@@ -149,7 +149,7 @@ def tile_routed_moe_kernel(tc, xT, w, b, gate, offs, out):
                 scales=scales[:, places],
                 in_=grouped[:, places, :].rearrange("p n t -> p (n t)"),
             )
-            for done, which in sorted(layout[first : first + count]):
+            for which, done in sorted((which, done) for done, which in layout[first : first + count]):
                 place = layout.index((done, which))
                 if done == 0:
                     sums[e, which] = psum.tile([P, C], F32, name=f"acc{which}")
@@ -182,22 +182,16 @@ def tile_routed_moe_kernel(tc, xT, w, b, gate, offs, out):
             if e == LAST:
                 nc.sync.dma_start(out[band(m), :], windows[m][:])
 
-        def first_pass(e, bands):
-            rounded("vector", e, 0, 0, 2)
-            multiply(e, 0, 0, 2)
-            rounded("scalar", e, 0, 2, 4)
-            held = w_raw[e, 0][:, :, band(0)]
-            for first, end in bands:
-                gated(e - 1, held[:, first:end, :], y[e - 1][:, first:end, :])
-                for m in range(first, end):
-                    scatter("scalar", e - 1, m, held[:, m, :])
+        def finish(e, first, end):
+            held = w_raw[e + 1, 0][:, :, band(0)]
+            gated(e, held[:, first:end, :], y[e][:, first:end, :])
+            return [(e, m, held[:, m, :]) for m in range(first, end)]
 
         open_expert(0)
         for a in range(2):
             rounded("scalar", 0, a, 0, 2)
             rounded("scalar", 0, a, 2, 4)
-        multiply(0, 0, 0, 2)
-        multiply(0, 0, 2, 4)
+            multiply(0, 0, 2 * a, 2 + 2 * a)
         rounded("vector", 0, 2, 0, 2)
         rounded("scalar", 0, 2, 2, 4)
         multiply(0, 1, 2, 4)
@@ -206,28 +200,41 @@ def tile_routed_moe_kernel(tc, xT, w, b, gate, offs, out):
             empty("scalar", 0, m, y[0][:, m, :])
 
         for e in range(1, LAST):
+            shared = e == LAST - 1
             open_expert(e)
-            first_pass(e, ((0, 2), (2, 4)))
+            rounded("vector", e, 0, 0, 2)
+            products = finish(e - 1, 0, 2)
+            if shared:
+                rounded("vector", e, 0, 2)
+            rounded("scalar", e, 0, 3 if shared else 2, 4)
+            for product in products + finish(e - 1, 2, 4):
+                scatter("scalar", *product)
+            multiply(e, 0, 0, 2)
             rounded("vector", e, 1, 0, 2)
             rounded("vector", e, 1, 2, 4)
             multiply(e, 0, 2, 4)
-            multiply(e, 1, 2, 2)
+            if shared:
+                multiply(e, 1, 2, 2)
             rounded("vector", e, 2, 0, 2)
-            rounded("vector", e, 2, 2, 4)
-            multiply(e, 2, 0, 2)
+            if shared:
+                rounded("vector", e, 2, 2)
+                rounded("scalar", e, 2, 3)
+                multiply(e, 2, 0, 2)
+            else:
+                rounded("vector", e, 2, 2, 4)
+                multiply(e, 1, 2, 4)
             multiply(e, 2, 2, 2)
             for m in range(M):
                 empty("scalar", e, m, y[e][:, m, :])
 
         e = LAST
         open_expert(e)
-        rounded("vector", e, 0, 0, 2)
-        rounded("vector", e, 0, 2)
-        rounded("scalar", e, 0, 3)
-        held = w_raw[e, 0][:, :, band(0)]
-        gated(e - 1, held[:, 0:3, :], y[e - 1][:, 0:3, :])
-        for m in range(3):
-            scatter("scalar", e - 1, m, held[:, m, :])
+        rounded("vector", e, 0, 0)
+        products = finish(e - 1, 0, 2)
+        rounded("vector", e, 0, 1)
+        rounded("scalar", e, 0, 2, 4)
+        for product in products:
+            scatter("scalar", *product)
         multiply(e, 0, 0, 2)
         rounded("vector", e, 1, 0, 2)
         for m in range(2):
@@ -235,6 +242,9 @@ def tile_routed_moe_kernel(tc, xT, w, b, gate, offs, out):
         multiply(e, 1, 0, 3)
         multiply(e, 2, 1, 3)
         empty("scalar", e, 0, y[e][:, 0, :])
+        later = w_raw[e, 2][:, 0:1, band(1)]
+        gated(e - 1, later, y[e - 1][:, 2:3, :])
+        scatter("scalar", e - 1, 2, later[:, 0, :])
         rounded("vector", e, 1, 2, 4)
         gated(e, y[e][:, 0:1, :], y[e][:, 0:1, :])
         spent = w_raw[e, 1][:, 0, band(3)]

@@ -32,8 +32,9 @@ X_COPIES = (("vector", 0, X_FIRST), ("scalar", X_FIRST, T - X_TAIL), ("vector", 
 
 HALF = N // 2
 LAST = E - 1
+EARLY = 96
 IN_ORDER = tuple((a, m) for a in range(A) for m in range(M))
-LAST_LAYOUT = ((0, 0), (0, 1), (1, 0), (1, 1), (2, 0), (2, 1), (0, 2), (0, 3), (2, 2), (1, 2), (1, 3), (2, 3))
+LAST_LAYOUT = ((0, 0), (0, 1), (1, 0), (1, 1), (2, 0), (2, 1), (0, 2), (0, 3), (1, 2), (1, 3), (2, 2), (2, 3))
 
 
 def round_and_group(nc, engine, grouped, raw):
@@ -213,16 +214,14 @@ def tile_routed_moe_kernel(tc, xT, w, b, gate, offs, out):
             rounded("vector", e, 1, 0, 2)
             rounded("vector", e, 1, 2, 4)
             multiply(e, 0, 2, 4)
-            if shared:
-                multiply(e, 1, 2, 2)
+            multiply(e, 1, 2, 2)
             rounded("vector", e, 2, 0, 2)
             if shared:
                 rounded("vector", e, 2, 2)
                 rounded("scalar", e, 2, 3)
-                multiply(e, 2, 0, 2)
             else:
                 rounded("vector", e, 2, 2, 4)
-                multiply(e, 1, 2, 4)
+            multiply(e, 2, 0, 2)
             multiply(e, 2, 2, 2)
             for m in range(M):
                 empty("scalar", e, m, y[e][:, m, :])
@@ -232,8 +231,9 @@ def tile_routed_moe_kernel(tc, xT, w, b, gate, offs, out):
         rounded("vector", e, 0, 0)
         products = finish(e - 1, 0, 2)
         rounded("vector", e, 0, 1)
-        rounded("scalar", e, 0, 2, 4)
-        for product in products:
+        rounded("vector", e, 0, 2)
+        rounded("scalar", e, 0, 3)
+        for product in products + finish(e - 1, 2, 3):
             scatter("scalar", *product)
         multiply(e, 0, 0, 2)
         rounded("vector", e, 1, 0, 2)
@@ -242,23 +242,21 @@ def tile_routed_moe_kernel(tc, xT, w, b, gate, offs, out):
         multiply(e, 1, 0, 3)
         multiply(e, 2, 1, 3)
         empty("scalar", e, 0, y[e][:, 0, :])
-        later = w_raw[e, 2][:, 0:1, band(1)]
-        gated(e - 1, later, y[e - 1][:, 2:3, :])
-        scatter("scalar", e - 1, 2, later[:, 0, :])
         rounded("vector", e, 1, 2, 4)
         gated(e, y[e][:, 0:1, :], y[e][:, 0:1, :])
         spent = w_raw[e, 1][:, 0, band(3)]
         empty("scalar", e, 1, spent)
         scatter("scalar", e, 0, y[e][:, 0, :])
+        multiply(e, 1, 2, 2)
         rounded("vector", e, 2, 2)
         rounded("vector", e, 2, 3)
-        multiply(e, 2, 2, 2)
-        multiply(e, 1, 3, 2)
-        late = w_raw[e, 2][:, 0:1, band(3)]
-        gated(e - 1, late, y[e - 1][:, 3:4, :])
+        late = w_raw[e, 2][:, 0, 3 * P - EARLY : 4 * P - EARLY]
+        for m, part in ((2, slice(0, EARLY)), (3, slice(EARLY, C))):
+            multiply(e, 2, m)
+            nc.vector.tensor_tensor(late[:, part], y[e - 1][:, 3, part], gates[:, band(e - 1)][:, part], MULT)
         scatter("vector", e, 1, spent)
         for m in (2, 3):
             empty("scalar", e, m, y[e][:, m, :])
-        scatter("scalar", e - 1, 3, late[:, 0, :])
+        scatter("scalar", e - 1, 3, late)
         for m in (2, 3):
             scatter("vector", e, m, y[e][:, m, :])

@@ -33,6 +33,7 @@ X_COPIES = (("vector", 0, X_FIRST), ("scalar", X_FIRST, T - X_TAIL), ("vector", 
 HALF = N // 2
 LAST = E - 1
 EARLY = 96
+CUT = HALF + 96
 IN_ORDER = tuple((a, m) for a in range(A) for m in range(M))
 LAST_LAYOUT = ((0, 0), (0, 1), (1, 0), (1, 1), (2, 0), (2, 1), (0, 2), (0, 3), (1, 2), (1, 3), (2, 2), (2, 3))
 
@@ -141,6 +142,11 @@ def tile_routed_moe_kernel(tc, xT, w, b, gate, offs, out):
             place = layout.index((a, first)) * P
             round_and_group(nc, engine, grouped[:, place : place + cols.stop - cols.start, :], w_raw[e, a][:, :, cols])
 
+        def rounded_columns(engine, e, a, lo, hi):
+            layout, grouped = stage[e][:2]
+            place = layout.index((a, lo // P)) * P + lo % P
+            round_and_group(nc, engine, grouped[:, place : place + hi - lo, :], w_raw[e, a][:, :, lo:hi])
+
         def multiply(e, a, m, count=1):
             layout, grouped, codes, scales = stage[e]
             first = layout.index((a, m))
@@ -215,25 +221,31 @@ def tile_routed_moe_kernel(tc, xT, w, b, gate, offs, out):
             rounded("vector", e, 1, 2, 4)
             multiply(e, 0, 2, 4)
             multiply(e, 1, 2, 2)
-            rounded("vector", e, 2, 0, 2)
             if shared:
+                rounded("vector", e, 2, 0)
+                rounded("vector", e, 2, 1)
+                multiply(e, 2, 0)
                 rounded("vector", e, 2, 2)
                 rounded("scalar", e, 2, 3)
+                multiply(e, 2, 1)
             else:
+                rounded("vector", e, 2, 0, 2)
                 rounded("vector", e, 2, 2, 4)
-            multiply(e, 2, 0, 2)
+                multiply(e, 2, 0, 2)
             multiply(e, 2, 2, 2)
             for m in range(M):
                 empty("scalar", e, m, y[e][:, m, :])
 
         e = LAST
+        gated(e - 1, y[e - 1][:, 0:1, :], y[e - 1][:, 0:1, :])
+        scatter("scalar", e - 1, 0, y[e - 1][:, 0, :])
         open_expert(e)
         rounded("vector", e, 0, 0)
-        products = finish(e - 1, 0, 2)
         rounded("vector", e, 0, 1)
-        rounded("vector", e, 0, 2)
-        rounded("scalar", e, 0, 3)
-        for product in products + finish(e - 1, 2, 3):
+        products = finish(e - 1, 1, 3)
+        rounded_columns("vector", e, 0, HALF, CUT)
+        rounded_columns("scalar", e, 0, CUT, N)
+        for product in products:
             scatter("scalar", *product)
         multiply(e, 0, 0, 2)
         rounded("vector", e, 1, 0, 2)

from contextlib import ExitStack

import concourse.mybir as mybir
from concourse.masks import make_identity

K, T, E, C, N = 1536, 768, 4, 128, 512
P = 128
PACK = 4
A = K // (P * PACK)
S = E * C
M = N // P

FLOPS = 2 * K * N * S
BYTES = 4 * (K * T + E * K * N + N * E + S + N * T) + 2 * P * (S // 16)

F32 = mybir.dt.float32
BF16 = mybir.dt.bfloat16
U32 = mybir.dt.uint32
U16 = mybir.dt.uint16
U8 = mybir.dt.uint8
FP8X4 = mybir.dt.float8_e4m3fn_x4
RELU = mybir.ActivationFunctionType.Relu
COPY = mybir.ActivationFunctionType.Copy
MULT = mybir.AluOpType.mult
ADD = mybir.AluOpType.add
MAX = mybir.AluOpType.max

X_FIRST = 256
X_QUANTISE = ((0, X_FIRST), (X_FIRST, T))
X_TAIL = T // 2 - X_FIRST
X_COPIES = (("vector", 0, X_FIRST), ("scalar", X_FIRST, T - X_TAIL), ("vector", T - X_TAIL, T))

HALF = N // 2
LAST = E - 1
EARLY = 96
CUT = HALF + 96
IN_ORDER = tuple((a, m) for a in range(A) for m in range(M))
LAST_LAYOUT = ((0, 0), (0, 1), (1, 0), (1, 1), (2, 0), (2, 1), (0, 2), (0, 3), (1, 2), (1, 3), (2, 2), (2, 3))


def round_and_group(nc, engine, grouped, raw):
    copy = nc.scalar.copy if engine == "scalar" else nc.vector.tensor_copy
    copy(
        out=grouped.rearrange("p (c i) (u v) -> p c u i v", i=4, v=2),
        in_=raw.rearrange("p (u v) (c i) -> p c u i v", i=4, v=2),
    )


def band(first, end=None):
    return slice(first * P, (first + 1 if end is None else end) * P)


def tile_routed_moe_kernel(tc, xT, w, b, gate, offs, out):
    nc = tc.nc
    with ExitStack() as ctx:
        keep = ctx.enter_context(tc.tile_pool(name="keep", bufs=1))
        xstage = ctx.enter_context(tc.tile_pool(name="xstage", bufs=2))
        wstage = ctx.enter_context(tc.tile_pool(name="wstage", bufs=2))
        psum = ctx.enter_context(tc.psum_pool(name="psum", bufs=2))

        x_rows = xT.rearrange("(a p t) n -> a p t n", p=P, t=PACK)
        w_rows = w.rearrange("e (a p t) n -> e a p t n", p=P, t=PACK)

        offsets = keep.tile([P, S // 16], U16, name="offsets")
        x_raw = [keep.tile([P, PACK, T], F32, name=f"x_raw{a}") for a in range(A)]
        x_codes = [keep.tile([P, T], U32, name=f"x_codes{a}", align_bytes=64) for a in range(A)]
        x_scales = keep.tile([P, T], U8, name="x_scales", align_bytes=64)
        s_codes = [keep.tile([P, S], U32, name=f"s_codes{a}", align_bytes=64) for a in range(A)]
        s_scales = keep.tile([P, S], U8, name="s_scales", align_bytes=64)
        bias = keep.tile([P, E, M], F32, name="bias")
        gates = keep.tile([P, S], F32, name="gates")
        windows = [keep.tile([P, T], F32, name=f"window{m}") for m in range(M)]
        w_raw = {(e, a): keep.tile([P, PACK, N], F32, name=f"w_raw{e}_{a}") for e in range(E) for a in range(A)}
        y = [keep.tile([P, M, C], F32, name=f"y{e}") for e in range(E)]

        gate_row = keep.tile([P, S], F32, name="gate_row")
        ones = keep.tile([P, P], F32, name="ones")
        b_rows = keep.tile([M, P, E], F32, name="b_rows")
        b_laid = keep.tile([P, E, P], F32, name="b_laid")
        identity = keep.tile([P, P], F32, name="identity")
        nc.gpsimd.memset(b_laid[:], 0.0)
        make_identity(nc, identity[:])
        nc.gpsimd.memset(gate_row[:], 0.0)
        nc.gpsimd.memset(x_scales[:], 0)
        nc.scalar.activation(out=ones[:], in_=gate_row[:, 0:P], func=RELU, bias=1.0, scale=1.0)

        for a in range(A):
            nc.sync.dma_start(x_raw[a][:], x_rows[a])
            if a == 0:
                nc.sync.dma_start(b_rows[:], b.rearrange("(m p) e -> m p e", p=P))
                nc.sync.dma_start(offsets[:], offs)
            if a == 1:
                nc.sync.dma_start(gate_row[0:1, :], gate[0:1, :])
        for e in range(LAST):
            for a in range(A):
                nc.sync.dma_start(w_raw[e, a][:], w_rows[e, a])
        nc.sync.dma_start(w_raw[LAST, 0][:], w_rows[LAST, 0])
        for cols in (band(0, 2), band(2, 4)):
            for a in (1, 2):
                nc.sync.dma_start(w_raw[LAST, a][:, :, cols], w_rows[LAST, a, :, :, cols])

        for m in range(M):
            nc.vector.memset(windows[m][:], 0.0)

        nc.vector.tensor_copy(b_laid[0:M], b_rows[:].rearrange("m p e -> m e p"))
        turned = psum.tile([P, E, M], F32, name="acc1")
        for e in range(E):
            nc.tensor.matmul(turned[:, e, :], b_laid[:, e, :], identity[:, 0:M], start=True, stop=True)
        nc.scalar.copy(bias[:], turned[:])

        spread = psum.tile([P, S], F32, name="acc0")
        nc.tensor.matmul(spread[:], ones[:], gate_row[:], start=True, stop=True)
        nc.scalar.copy(gates[:], spread[:])

        for a in range(A):
            x_grouped = xstage.tile([P, T, PACK], BF16, name="x_grouped", align_bytes=64)
            for engine, lo, hi in X_COPIES:
                round_and_group(nc, engine, x_grouped[:, lo:hi, :], x_raw[a][:, :, lo:hi])
            for lo, hi in X_QUANTISE:
                nc.vector.quantize_mx(
                    out=x_codes[a][:, lo:hi].bitcast(FP8X4),
                    scales=x_scales[PACK * a : P, lo:hi],
                    in_=x_grouped[:, lo:hi, :].rearrange("p n t -> p (n t)"),
                )
            nc.vector.tensor_copy(s_codes[a][:], x_codes[a][:].indirect(offsets[:]))
        nc.vector.tensor_copy(s_scales[:], x_scales[:].indirect(offsets[:]))

        stage = {}
        sums = {}

        def open_expert(e):
            stage[e] = (
                LAST_LAYOUT if e == LAST else IN_ORDER,
                wstage.tile([P, A * N, PACK], BF16, name="w_grouped", align_bytes=64),
                wstage.tile([P, A * N], U32, name="w_codes", align_bytes=64),
                wstage.tile([P, A * N], U8, name="w_scales", align_bytes=64),
            )

        def rounded(engine, e, a, first, end=None):
            layout, grouped = stage[e][:2]
            cols = band(first, end)
            place = layout.index((a, first)) * P
            round_and_group(nc, engine, grouped[:, place : place + cols.stop - cols.start, :], w_raw[e, a][:, :, cols])

        def rounded_columns(engine, e, a, lo, hi):
            layout, grouped = stage[e][:2]
            place = layout.index((a, lo // P)) * P + lo % P
            round_and_group(nc, engine, grouped[:, place : place + hi - lo, :], w_raw[e, a][:, :, lo:hi])

        def multiply(e, a, m, count=1):
            layout, grouped, codes, scales = stage[e]
            first = layout.index((a, m))
            places = band(first, first + count)
            nc.vector.quantize_mx(
                out=codes[:, places].bitcast(FP8X4),
                scales=scales[:, places],
                in_=grouped[:, places, :].rearrange("p n t -> p (n t)"),
            )
            for which, done in sorted((which, done) for done, which in layout[first : first + count]):
                place = layout.index((done, which))
                if done == 0:
                    sums[e, which] = psum.tile([P, C], F32, name=f"acc{which}")
                nc.tensor.matmul_mx(
                    out=sums[e, which][:],
                    lhsT=codes[:, band(place)].bitcast(FP8X4),
                    lhsT_scale=scales[:, band(place)],
                    rhs=s_codes[done][:, band(e)].bitcast(FP8X4),
                    rhs_scale=s_scales[PACK * done : P, band(e)],
                    start=(done == 0),
                    stop=(done == A - 1),
                )

        def empty(engine, e, m, into):
            if engine == "vector":
                nc.vector.tensor_scalar(into, sums[e, m][:], bias[:, e, m : m + 1], 0.0, ADD, MAX)
            else:
                nc.scalar.activation(out=into, in_=sums[e, m][:], func=RELU, bias=bias[:, e, m : m + 1], scale=1.0)

        def gated(e, into, values):
            weights = gates[:, band(e)].unsqueeze(1).to_broadcast(list(values.shape))
            nc.vector.tensor_tensor(into, values, weights, MULT)

        def scatter(engine, e, m, values):
            window = windows[m][:].indirect(offsets[:, e * C // 16 : (e + 1) * C // 16])
            if engine == "vector":
                nc.vector.tensor_tensor(window, values, gates[:, band(e)], MULT)
            else:
                nc.scalar.activation(window, values, COPY)
            if e == LAST:
                nc.sync.dma_start(out[band(m), :], windows[m][:])

        def finish(e, first, end):
            held = w_raw[e + 1, 0][:, :, band(0)]
            gated(e, held[:, first:end, :], y[e][:, first:end, :])
            return [(e, m, held[:, m, :]) for m in range(first, end)]

        open_expert(0)
        for a in range(2):
            rounded("scalar", 0, a, 0, 2)
            rounded("scalar", 0, a, 2, 4)
            multiply(0, 0, 2 * a, 2 + 2 * a)
        rounded("vector", 0, 2, 0, 2)
        rounded("scalar", 0, 2, 2, 4)
        multiply(0, 1, 2, 4)
        multiply(0, 2, 2, 2)
        for m in range(M):
            empty("scalar", 0, m, y[0][:, m, :])

        for e in range(1, LAST):
            shared = e == LAST - 1
            open_expert(e)
            rounded("vector", e, 0, 0, 2)
            products = finish(e - 1, 0, 2)
            if shared:
                rounded("vector", e, 0, 2)
            rounded("scalar", e, 0, 3 if shared else 2, 4)
            for product in products + finish(e - 1, 2, 4):
                scatter("scalar", *product)
            multiply(e, 0, 0, 2)
            rounded("vector", e, 1, 0, 2)
            rounded("vector", e, 1, 2, 4)
            multiply(e, 0, 2, 4)
            multiply(e, 1, 2, 2)
            if shared:
                rounded("vector", e, 2, 0)
                rounded("vector", e, 2, 1)
                multiply(e, 2, 0)
                rounded("vector", e, 2, 2)
                rounded("scalar", e, 2, 3)
                multiply(e, 2, 1)
            else:
                rounded("vector", e, 2, 0, 2)
                rounded("vector", e, 2, 2, 4)
                multiply(e, 2, 0, 2)
            multiply(e, 2, 2, 2)
            for m in range(M):
                empty("scalar", e, m, y[e][:, m, :])

        e = LAST
        gated(e - 1, y[e - 1][:, 0:1, :], y[e - 1][:, 0:1, :])
        scatter("scalar", e - 1, 0, y[e - 1][:, 0, :])
        open_expert(e)
        rounded("vector", e, 0, 0)
        rounded("vector", e, 0, 1)
        products = finish(e - 1, 1, 3)
        rounded_columns("vector", e, 0, HALF, CUT)
        rounded_columns("scalar", e, 0, CUT, N)
        for product in products:
            scatter("scalar", *product)
        multiply(e, 0, 0, 2)
        rounded("vector", e, 1, 0, 2)
        for m in range(2):
            rounded("vector", e, 2, m)
        multiply(e, 1, 0, 3)
        multiply(e, 2, 1, 3)
        empty("scalar", e, 0, y[e][:, 0, :])
        rounded("vector", e, 1, 2, 4)
        gated(e, y[e][:, 0:1, :], y[e][:, 0:1, :])
        spent = w_raw[e, 1][:, 0, band(3)]
        empty("scalar", e, 1, spent)
        scatter("scalar", e, 0, y[e][:, 0, :])
        multiply(e, 1, 2, 2)
        rounded("vector", e, 2, 2)
        rounded("vector", e, 2, 3)
        late = w_raw[e, 2][:, 0, 3 * P - EARLY : 4 * P - EARLY]
        for m, part in ((2, slice(0, EARLY)), (3, slice(EARLY, C))):
            multiply(e, 2, m)
            nc.vector.tensor_tensor(late[:, part], y[e - 1][:, 3, part], gates[:, band(e - 1)][:, part], MULT)
        scatter("vector", e, 1, spent)
        for m in (2, 3):
            empty("scalar", e, m, y[e][:, m, :])
        scatter("scalar", e - 1, 3, late)
        for m in (2, 3):
            scatter("vector", e, m, y[e][:, m, :])
